import numpy as np, ml_dtypes
CORES = [113,118,241,246]
N = 4
R, T, B = 16384, 4096, 512
def entries(a): return a.T.reshape(-1)
def pack(v, P): return np.ascontiguousarray(np.asarray(v, np.int32).reshape(-1, P).T)
def lists(rng, how):
    I = rng.integers(0, N * R, (N, T)); E = np.sort(rng.integers(0, T + 1, (N, B)), axis=1)
    if how == "void":
        E = np.zeros((N, B), np.int64)
        for r in range(N): k = np.sort(1 + rng.permutation(B - 2)[:6]); c = np.sort(1 + rng.permutation(T)[:6]); E[r] = np.concatenate([[0], c])[np.searchsorted(k, np.arange(B), side="right")]
        E[rng.integers(N)] = 0
    if how == "one":
        p = rng.permutation(N); z = rng.integers(0, B, N); z[p[0]] = 0; z[p[1]] = B - 1; E = np.where(np.arange(B)[None, :] < z[:, None], 0, T)
        I[p[::2]] = R * p[1] + I[p[::2]] % R
    if how == "single": E = np.broadcast_to(1 + np.arange(B), (N, B)).copy()
    if how == "hotrank": I = R * int(rng.integers(N)) + rng.integers(0, R, (N, T))
    if how == "edge": I = R * rng.integers(0, N, (N, T)) + np.where(rng.random((N, T)) < 0.5, 0, R - 1); E[:, -1] = T
    return {"idx": np.stack([pack(i, 16) for i in I]), "end": np.stack([pack(v, 16) for v in E])}
def setup_inputs(rng):
    return dict({"tab": rng.standard_normal((N, 128, R), dtype=np.float32).astype(ml_dtypes.bfloat16)}, **lists(rng, "uniform"))
def setup_inputs_edge(rng):
    d = setup_inputs(rng); d.update(lists(rng, "edge"))
    for k in ("tab",): d[k] = (d[k].astype(np.float32) * 1048576.0).astype(d[k].dtype)
    return d
def setup_inputs_hotrank(rng):
    d = setup_inputs(rng); d.update(lists(rng, "hotrank"))
    for k in ("tab",): d[k] = (d[k].astype(np.float32) * (1 / 1024.0)).astype(d[k].dtype)
    return d
def setup_inputs_one(rng):
    d = setup_inputs(rng); d.update(lists(rng, "one"))
    return d
def setup_inputs_single(rng):
    d = setup_inputs(rng); d.update(lists(rng, "single"))
    return d
def setup_inputs_void(rng):
    d = setup_inputs(rng); d.update(lists(rng, "void"))
    return d
def check_inputs(x):
    bad = []
    if x["idx"].min() < 0 or x["idx"].max() >= N * R: bad.append("idx out of range")
    if x["end"].min() < 0 or x["end"].max() >= T + 1: bad.append("end out of range")
    if any((np.diff(entries(a)) < 0).any() for a in x["end"]): bad.append("end falls")
    t = x["tab"].astype(np.float32)
    if t.min() < -1e30 or t.max() > 1e30: bad.append("tab beyond -1e30 to 1e30")
    return bad
def reference(tab, idx, end):
    A = np.concatenate(list(tab), axis=1)
    y = np.zeros((N, 128, B), tab.dtype)
    for r in range(N):
        G = A[:, entries(idx[r])]; c = np.concatenate([[0], entries(end[r])])
        for b in range(B):
            if c[b + 1] > c[b]: y[r][:, b] = G[:, c[b]:c[b + 1]].max(axis=1)
    return {"y": y}

@@ -1,0 +1,229 @@
+from concourse.bass import DstId, RemoteDMATransfer
+from concourse.mybir import dt, AluOpType, AxisListType, ActivationFunctionType
+
+N, R, TL, B = 4, 16384, 4096, 512
+LW = TL // 16 + 2 * (B // 16)
+C0, C1, C2 = 0, TL // 16, TL // 16 + B // 16
+PAD = 16
+WW = R + 2 * PAD
+NEV = 110
+
+SCRATCH = {
+    "lraw": ("sbuf", [128, LW], "int32"),
+    "lf": ("sbuf", [128, LW], "float32"),
+    "flag": ("sbuf", [128, B // 16], "float32"),
+    "spare": ("sbuf", [128, B // 16], "float32"),
+    "ones": ("sbuf", [128, 128], "float32"),
+    "rep": ("sbuf", [128, 128], "float32"),
+    "ps": ("psum", [128, 512], "float32"),
+    "lists": ("sbuf", [128, N * LW], "uint16"),
+    "offs": ("sbuf", [128, N * (TL // 16)], "uint16"),
+    "low0": ("sbuf", [128, B], "bfloat16"),
+    "low": ("sbuf", [128, B], "bfloat16"),
+    "win": ("sbuf", [128, WW], "bfloat16"),
+    "msk": ("sbuf", [128, N * (TL + B)], "bfloat16"),
+    "gat": ("sbuf", [128, N * TL], "bfloat16"),
+    "scn": ("sbuf", [128, N * (TL + 16)], "bfloat16"),
+    "part": ("sbuf", [128, N * B], "bfloat16"),
+    "land": ("sbuf", [128, N * B], "bfloat16"),
+    "acc": ("sbuf", [128, 2 * B], "bfloat16"),
+    "yt": ("sbuf", [128, B], "bfloat16"),
+}
+SEMAPHORES = (["e%d" % i for i in range(NEV)] + ["al%d" % i for i in range(N)] + ["ap%d" % i for i in range(N)]
+              + ["sent"])
+
+
+def rank_program(g, core, T, topo):
+    p = T.rank_of(core)
+    if p is None:
+        return
+    v, s, te, sy = g.vector, g.scalar, g.tensor, g.sync
+    OP, COPY = AluOpType, ActivationFunctionType.Copy
+
+    n_ev, waited, all_ev, seen = [0], {}, [], {}
+
+    def ev(inst, n=1):
+        sem = T.sem["e%d" % n_ev[0]]
+        n_ev[0] += 1
+        inst.then_inc(sem, n)
+        e = (n_ev[0], sem, n)
+        all_ev.append(e)
+        return e
+
+    def need(name, *evs):
+        q = {"v": v, "s": s, "t": te, "y": sy, "g": g}[name]
+        for e in evs:
+            if (name, e[0]) not in seen:
+                seen[(name, e[0])] = 1
+                waited[e[0]] = 1
+                q.wait_ge(e[1], e[2])
+
+    others = [r for r in range(N) if r != p]
+    far = [r for r in others if topo.host(T.cores[r]) != topo.host(core)]
+    far = sorted(far, key=lambda r: topo.die(T.cores[r]) != topo.die(core))
+    near = [r for r in others if r not in far]
+    order = far + near
+
+    def lst(r, a, b):
+        return T.lists[:, r * LW + a:r * LW + b]
+
+    e_m0 = ev(v.memset(T.lraw[0:16, C2:LW], 0))
+    e_ones = ev(v.memset(T.ones[0:16, :], 1.0))
+    e_ld = [ev(sy.dma_start(T.lraw[0:16, 0:C1], T.idx[:]), 16),
+            ev(sy.dma_start(T.lraw[0:16, C1:C2], T.end[:]), 16)]
+    e_tab = [ev(sy.dma_start(T.win[:, PAD:PAD + R // 2], T.tab[:, 0:R // 2]), 16)]
+    need("s", e_m0)
+    e_ld.append(ev(s.dma_start(T.lraw[1:16, C2:LW], T.end[0:15, :]), 16))
+    e_ld.append(ev(s.dma_start(T.lraw[0:1, C2 + 1:LW], T.end[15:16, 0:B // 16 - 1]), 16))
+    e_tab.append(ev(s.dma_start(T.win[:, PAD + R // 2:PAD + R], T.tab[:, R // 2:R]), 16))
+
+    e_sp = ev(g.iota(T.spare[0:16, :], [[16, B // 16]], TL, 1, allow_small_or_imprecise_dtypes=True))
+    need("g", e_ones)
+    e_rep = ev(g.affine_select(T.rep[0:16, :], T.ones[0:16, :], [[0, 8], [1, 16]], OP.is_equal, 0.0, 0, -1))
+
+    MW = TL + B
+
+    def mz(r):
+        return T.msk[:, r * MW:r * MW + TL]
+    e_low0 = ev(v.memset(T.low0[:], -9e29))
+    e_mz = {p: ev(v.memset(mz(p), 0.0))}
+    e_mz[order[0]] = None
+    need("s", e_mz[p])
+    e_mz[order[0]] = ev(s.activation(mz(order[0]), mz(p), COPY))
+    need("s", e_mz[order[0]])
+    e_mz[order[1]] = ev(s.activation(mz(order[1]), mz(order[0]), COPY))
+    need("v", e_low0)
+    e_low = ev(v.tensor_scalar(T.low[:], T.low0[:], 1e6, None, OP.mult))
+    e_pad = [ev(v.tensor_scalar(T.win[:, 0:PAD], T.low0[:, 0:PAD], 1e6, None, OP.mult)),
+             ev(v.tensor_scalar(T.win[:, PAD + R:WW], T.low0[:, 0:PAD], 1e6, None, OP.mult))]
+
+    need("v", *e_ld)
+    e_c = ev(v.tensor_copy(T.lf[0:16, :], T.lraw[0:16, :]))
+    E, EP, F, D = T.lf[0:16, C1:C2], T.lf[0:16, C2:LW], T.flag[0:16, :], T.spare[0:16, :]
+    need("v", e_c, e_sp)
+    e_f = ev(v.tensor_tensor(F, E, EP, OP.is_gt))
+    need("v", e_f)
+    e_1 = ev(v.tensor_tensor(E, E, F, OP.mult))
+    e_2 = ev(v.tensor_tensor(EP, EP, D, OP.subtract))
+    need("v", e_2)
+    e_3 = ev(v.tensor_tensor(EP, EP, F, OP.mult))
+    need("v", e_3)
+    e_4 = ev(v.tensor_tensor(EP, EP, D, OP.add))
+    need("t", e_rep, e_c, e_1, e_4)
+    e_ps = ev(te.matmul(T.ps[:, 0:LW], T.rep[0:16, :], T.lf[0:16, :], start=True, stop=True))
+    need("v", e_ps)
+    e_u = ev(v.tensor_copy(lst(p, 0, LW), T.ps[:, 0:LW]))
+
+    mask = 0xFFFF
+    for r in others:
+        mask &= topo.mask(core, T.cores[r])
+    ids = []
+    for r in others:
+        rid, pid = topo.addr(T.cores[r], core)
+        ids.append(DstId(rid=rid, pnc=pid))
+    nsent = [0]
+    need("g", e_u)
+    g.remote_dma_fused([RemoteDMATransfer(srcs=[lst(p, 0, LW)], dsts=[lst(p, 0, LW) for r in others], dst_ids=ids,
+                                          dma_engine_mask=mask, remote_sem=T.sem["al%d" % p])], local_sem=T.sem.sent)
+    nsent[0] += bin(mask).count("1")
+    e_mz[order[2]] = ev(g.iota(mz(order[2]), [[0, TL]], 0, 0, allow_small_or_imprecise_dtypes=True))
+
+    e_off, e_msk = {}, {}
+
+    def clip(r):
+        if r == p:
+            need("v", e_u)
+        else:
+            v.wait_ge(T.sem["al%d" % r], bin(mask).count("1"))
+        e_off[r] = ev(v.tensor_scalar(T.offs[:, r * C1:(r + 1) * C1], lst(r, C0, C1), float(PAD - R * p), float(PAD + R),
+                                      OP.add, OP.min))
+
+    def starts(r):
+        need("v", e_mz[r], e_low)
+        if r == p:
+            need("v", e_mz[order[0]])
+        if r == order[0]:
+            need("v", e_mz[order[1]])
+        e_msk[r] = ev(v.tensor_copy(T.msk[:, r * MW:(r + 1) * MW].indirect(lst(r, C2, LW)), T.low[:]))
+
+    SW = TL + 16
+    e_z = {}
+    for r in range(N):
+        e_z[r] = ev(v.memset(T.scn[:, r * SW + 15:r * SW + 16], 0.0))
+
+    CH = [0, 1024, 2048, 3072, 4096]
+    e_g, e_s, e_p = {}, {}, {}
+
+    def gath(name, r, c):
+        a, b = CH[c], CH[c + 1]
+        need(name, e_off[r], *e_tab, *e_pad)
+        out = T.gat[:, r * TL + a:r * TL + b]
+        src = T.win[:].indirect(T.offs[:, r * C1 + a // 16:r * C1 + b // 16])
+        e_g[(r, c)] = ev(v.tensor_copy(out, src) if name == "v" else s.activation(out, src, COPY))
+
+    def scan(r, c):
+        a, b = CH[c], CH[c + 1]
+        need("v", e_g[(r, c)], e_msk[r])
+        o = r * SW + 16
+        init = -9e29
+        if c:
+            need("v", e_s[(r, c - 1)])
+            init = T.scn[:, o + a - 1:o + a]
+        e_s[(r, c)] = ev(v.tensor_tensor_scan(T.scn[:, o + a:o + b], T.msk[:, r * MW + a:r * MW + b],
+                                              T.gat[:, r * TL + a:r * TL + b], init, OP.add, OP.max))
+
+    def bags(r):
+        return T.scn[:, r * SW + 15:(r + 1) * SW].indirect(lst(r, C1, C2))
+
+    def extract(r):
+        need("v", e_s[(r, len(CH) - 2)], e_z[r])
+        e_p[r] = ev(v.tensor_copy(T.part[:, r * B:(r + 1) * B], bags(r)))
+
+    def send(r):
+        m = topo.mask(core, T.cores[r])
+        rid, pid = topo.addr(T.cores[r], core)
+        need("g", e_p[r])
+        g.remote_dma(out_ap=T.land[:, p * B:(p + 1) * B], in_ap=T.part[:, r * B:(r + 1) * B], remote_sem=T.sem["ap%d" % p],
+                     local_sem=T.sem.sent, pid=pid, routing_id=rid, dma_engine_mask=m)
+        nsent[0] += bin(m).count("1")
+
+    def landed(r):
+        v.wait_ge(T.sem["ap%d" % r], bin(topo.mask(T.cores[r], core)).count("1"))
+        return T.land[:, r * B:(r + 1) * B]
+
+    f1, f2, nr = order
+    clip(p)
+    starts(p)
+    clip(f1), clip(f2), clip(nr)
+    starts(f1), starts(f2)
+
+    gath("s", p, 0)
+    for r in order:
+        for c in range(3):
+            gath("s", r, c)
+    gath("s", p, 1), gath("s", p, 2)
+
+    gath("v", p, 3), gath("v", f1, 3)
+    scan(p, 0)
+    scan(f1, 0), scan(f1, 1)
+    gath("v", f2, 3)
+    scan(f1, 2), scan(f1, 3), extract(f1), send(f1)
+    starts(nr)
+    scan(f2, 0), scan(f2, 1)
+    gath("v", nr, 3)
+    scan(f2, 2), scan(f2, 3), extract(f2), send(f2)
+    scan(nr, 0), scan(nr, 1), scan(nr, 2), scan(nr, 3), extract(nr), send(nr)
+    e_a = ev(v.tensor_tensor(T.acc[:, 0:B], landed(f1), landed(f2), OP.max))
+    scan(p, 1)
+    need("v", e_a)
+    e_b = ev(v.tensor_tensor(T.acc[:, B:2 * B], landed(nr), T.acc[:, 0:B], OP.max))
+    scan(p, 2), scan(p, 3)
+    need("v", e_b, e_s[(p, 3)], e_z[p])
+    e_y = ev(v.tensor_tensor(T.yt[:], bags(p), T.acc[:, B:2 * B], OP.max))
+    need("y", e_y)
+    e_o = ev(sy.dma_start(T.y[:], T.yt[:]), 16)
+    need("y", e_o)
+    g.wait_ge(T.sem.sent, nsent[0])
+    for e in all_ev:
+        if e[0] not in waited:
+            need("g", e)

@@ -2,45 +2,72 @@ from concourse.bass import DstId, RemoteDMATransfer
 from concourse.mybir import dt, AluOpType, AxisListType, ActivationFunctionType
 
 N, R, TL, B = 4, 16384, 4096, 512
-LW = TL // 16 + 2 * (B // 16)
-C0, C1, C2 = 0, TL // 16, TL // 16 + B // 16
+WORLD = 256
+TC, BC = TL // 16, B // 16
 PAD = 16
 WW = R + 2 * PAD
-NEV = 110
+MW = TL + B
+SW = TL + 16
+NEV = 100
+FAR = [0, 1024, 2048, 3072, 4096]
+NEAR = [0, 1024, 2048, 3072, 4096]
+OWN = [0, 768, 1792, 2816, 3584, 4096]
 
 SCRATCH = {
-    "lraw": ("sbuf", [128, LW], "int32"),
-    "lf": ("sbuf", [128, LW], "float32"),
-    "flag": ("sbuf", [128, B // 16], "float32"),
-    "spare": ("sbuf", [128, B // 16], "float32"),
+    "lraw": ("sbuf", [128, TC + 2 * BC], "int32"),
+    "lf": ("sbuf", [128, TC + 2 * BC], "float32"),
+    "flag": ("sbuf", [128, BC], "float32"),
+    "spare": ("sbuf", [128, BC], "float32"),
     "ones": ("sbuf", [128, 128], "float32"),
     "rep": ("sbuf", [128, 128], "float32"),
     "ps": ("psum", [128, 512], "float32"),
-    "lists": ("sbuf", [128, N * LW], "uint16"),
-    "offs": ("sbuf", [128, N * (TL // 16)], "uint16"),
+    "ps2": ("psum", [128, 512], "float32"),
+    "lists": ("sbuf", [128, N * TC], "uint16"),
+    "cuts": ("sbuf", [128, N * 2 * BC], "uint16"),
+    "offs": ("sbuf", [128, N * TC], "uint16"),
     "low0": ("sbuf", [128, B], "bfloat16"),
     "low": ("sbuf", [128, B], "bfloat16"),
     "win": ("sbuf", [128, WW], "bfloat16"),
-    "msk": ("sbuf", [128, N * (TL + B)], "bfloat16"),
+    "msk": ("sbuf", [128, 2 * MW], "bfloat16"),
     "gat": ("sbuf", [128, N * TL], "bfloat16"),
-    "scn": ("sbuf", [128, N * (TL + 16)], "bfloat16"),
-    "part": ("sbuf", [128, N * B], "bfloat16"),
-    "land": ("sbuf", [128, N * B], "bfloat16"),
-    "acc": ("sbuf", [128, 2 * B], "bfloat16"),
+    "scn": ("sbuf", [128, 2 * SW], "bfloat16"),
+    "part": ("sbuf", [128, 2 * B], "bfloat16"),
+    "landn": ("sbuf", [128, B], "bfloat16"),
+    "landf": ("sbuf", [128, B], "bfloat16"),
+    "acc": ("sbuf", [128, B], "bfloat16"),
     "yt": ("sbuf", [128, B], "bfloat16"),
 }
-SEMAPHORES = (["e%d" % i for i in range(NEV)] + ["al%d" % i for i in range(N)] + ["ap%d" % i for i in range(N)]
-              + ["sent"])
+SEMAPHORES = (["e%d" % i for i in range(NEV)] + ["al%d" % i for i in range(N)] + ["ac%d" % i for i in range(N)]
+              + ["ag%d" % i for i in range(8)] + ["an", "af", "sent"])
+
+
+def engines(mask):
+    return bin(mask).count("1")
 
 
 def rank_program(g, core, T, topo):
-    p = T.rank_of(core)
-    if p is None:
+    def helper_of(r):
+        c0 = T.cores[r]
+        return [c for c in range(WORLD) if topo.host(c) == topo.host(c0) and topo.chip(c) == topo.chip(c0)
+                and topo.die(c) == topo.die(c0) and T.rank_of(c) is None][0]
+
+    helper = [helper_of(r) for r in range(N)]
+    if core not in T.cores and core not in helper:
         return
+    is_rank = core in T.cores
+    p = T.rank_of(core) if is_rank else helper.index(core)
+
+    def around(q):
+        others = [r for r in range(N) if r != q]
+        fa = [r for r in others if topo.host(T.cores[r]) != topo.host(T.cores[q])]
+        fa = sorted(fa, key=lambda r: topo.die(T.cores[r]) == topo.die(T.cores[q]))
+        return fa + [r for r in others if r not in fa]
+
+    f1, f2, nr = around(p)
     v, s, te, sy = g.vector, g.scalar, g.tensor, g.sync
     OP, COPY = AluOpType, ActivationFunctionType.Copy
 
-    n_ev, waited, all_ev, seen = [0], {}, [], {}
+    n_ev, waited, all_ev, seen, nsent = [0], {}, [], {}, [0]
 
     def ev(inst, n=1):
         sem = T.sem["e%d" % n_ev[0]]
@@ -58,172 +85,227 @@ def rank_program(g, core, T, topo):
                 waited[e[0]] = 1
                 q.wait_ge(e[1], e[2])
 
-    others = [r for r in range(N) if r != p]
-    far = [r for r in others if topo.host(T.cores[r]) != topo.host(core)]
-    far = sorted(far, key=lambda r: topo.die(T.cores[r]) != topo.die(core))
-    near = [r for r in others if r not in far]
-    order = far + near
+    def finish():
+        g.wait_ge(T.sem.sent, nsent[0])
+        for e in all_ev:
+            if e[0] not in waited:
+                need("g", e)
 
-    def lst(r, a, b):
-        return T.lists[:, r * LW + a:r * LW + b]
+    def common(src, dsts):
+        m = 0xFFFF
+        for d in dsts:
+            m &= topo.mask(src, d)
+        return m
 
-    e_m0 = ev(v.memset(T.lraw[0:16, C2:LW], 0))
+    def put(dsts, sem, ap, mask):
+        ids = []
+        for d in dsts:
+            rid, pid = topo.addr(d, core)
+            ids.append(DstId(rid=rid, pnc=pid))
+        g.remote_dma_fused([RemoteDMATransfer(srcs=[ap], dsts=[ap for d in dsts], dst_ids=ids, dma_engine_mask=mask,
+                                              remote_sem=T.sem[sem])], local_sem=T.sem.sent)
+        nsent[0] += engines(mask)
+
+    def send(dst, sem, out, in_, mask):
+        rid, pid = topo.addr(dst, core)
+        g.remote_dma(out_ap=out, in_ap=in_, remote_sem=T.sem[sem], local_sem=T.sem.sent, pid=pid, routing_id=rid,
+                     dma_engine_mask=mask)
+        nsent[0] += engines(mask)
+
+    def cut_users(r):
+        a, b, c = around(r)
+        return [T.cores[c], helper[a], helper[b]]
+
+    def cut_mask(r):
+        return common(T.cores[r], cut_users(r))
+
+    def list_mask(r):
+        return common(T.cores[r], [T.cores[q] for q in range(N) if q != r])
+
+    def ends(r):
+        return T.cuts[:, 2 * BC * r:2 * BC * r + BC]
+
+    def starts(r):
+        return T.cuts[:, 2 * BC * r + BC:2 * BC * (r + 1)]
+
+    def mz(k, a=0, b=TL):
+        return T.msk[:, k * MW + a:k * MW + b]
+
+    def mark(k, r):
+        return ev(v.tensor_copy(T.msk[:, k * MW:(k + 1) * MW].indirect(starts(r)), T.low[:]))
+
+    def scan(k, r, a, b, deps, last):
+        need("v", *deps)
+        o = k * SW + 16
+        init = -9e29
+        if a:
+            need("v", last)
+            init = T.scn[:, o + a - 1:o + a]
+        return ev(v.tensor_tensor_scan(T.scn[:, o + a:o + b], mz(k, a, b), T.gat[:, r * TL + a:r * TL + b], init,
+                                       OP.add, OP.max))
+
+    def bags(k, r):
+        return T.scn[:, k * SW + 15:(k + 1) * SW].indirect(ends(r))
+
+    def low_columns():
+        e = ev(v.memset(T.low0[:], -9e29))
+        need("v", e)
+        return ev(v.tensor_scalar(T.low[:], T.low0[:], 1e6, None, OP.mult))
+
+    def piece(r, c):
+        return "ag%d" % (4 * [f1, f2].index(r) + c)
+
+    to_helper = topo.mask(T.cores[p], helper[p])
+
+    if not is_rank:
+        rank_core = T.cores[p]
+        mate = helper[nr]
+        pm = common(core, [T.cores[f2], mate])
+        mate_pm = common(mate, [T.cores[f1], core])
+        e_z = [ev(v.memset(T.scn[:, k * SW + 15:k * SW + 16], 0.0)) for k in range(2)]
+        e_low = low_columns()
+        e_m = [ev(v.memset(mz(k), 0.0)) for k in range(2)]
+        e_k = []
+        for k, r in enumerate((f1, f2)):
+            v.wait_ge(T.sem["ac%d" % r], engines(cut_mask(r)))
+            need("v", e_m[k], e_low)
+            e_k.append(mark(k, r))
+        for k, r in enumerate((f1, f2)):
+            last = None
+            for c in range(len(FAR) - 1):
+                v.wait_ge(T.sem[piece(r, c)], engines(to_helper))
+                last = scan(k, r, FAR[c], FAR[c + 1], [e_k[k]], last)
+            need("v", last, e_z[k])
+            out = T.part[:, k * B:(k + 1) * B]
+            if k == 0:
+                e_p = ev(v.tensor_copy(out, bags(k, r)))
+                need("g", e_p)
+                send(mate, "an", T.landn[:], out, pm)
+            else:
+                v.wait_ge(T.sem.an, engines(mate_pm))
+                e_p = ev(v.tensor_tensor(out, bags(k, r), T.landn[:], OP.max))
+                need("g", e_p)
+                send(T.cores[r], "af", T.landf[:], out, pm)
+        finish()
+        return
+
+    LE, LP = TC, TC + BC
+    e_m0 = ev(v.memset(T.lraw[0:16, LP:LP + BC], 0))
     e_ones = ev(v.memset(T.ones[0:16, :], 1.0))
-    e_ld = [ev(sy.dma_start(T.lraw[0:16, 0:C1], T.idx[:]), 16),
-            ev(sy.dma_start(T.lraw[0:16, C1:C2], T.end[:]), 16)]
+    e_idx = ev(sy.dma_start(T.lraw[0:16, 0:TC], T.idx[:]), 16)
+    e_end = [ev(sy.dma_start(T.lraw[0:16, LE:LP], T.end[:]), 16)]
     e_tab = [ev(sy.dma_start(T.win[:, PAD:PAD + R // 2], T.tab[:, 0:R // 2]), 16)]
     need("s", e_m0)
-    e_ld.append(ev(s.dma_start(T.lraw[1:16, C2:LW], T.end[0:15, :]), 16))
-    e_ld.append(ev(s.dma_start(T.lraw[0:1, C2 + 1:LW], T.end[15:16, 0:B // 16 - 1]), 16))
+    e_end.append(ev(s.dma_start(T.lraw[1:16, LP:LP + BC], T.end[0:15, :]), 16))
+    e_end.append(ev(s.dma_start(T.lraw[0:1, LP + 1:LP + BC], T.end[15:16, 0:BC - 1]), 16))
     e_tab.append(ev(s.dma_start(T.win[:, PAD + R // 2:PAD + R], T.tab[:, R // 2:R]), 16))
 
-    e_sp = ev(g.iota(T.spare[0:16, :], [[16, B // 16]], TL, 1, allow_small_or_imprecise_dtypes=True))
     need("g", e_ones)
     e_rep = ev(g.affine_select(T.rep[0:16, :], T.ones[0:16, :], [[0, 8], [1, 16]], OP.is_equal, 0.0, 0, -1))
+    e_sp = ev(g.iota(T.spare[0:16, :], [[16, BC]], TL, 1, allow_small_or_imprecise_dtypes=True))
+    H = TL // 2
+    e_mz = [ev(v.memset(mz(0, 0, H), 0.0))]
+    need("s", e_mz[0])
+    e_mz.append(ev(s.activation(mz(0, H, TL), mz(0, 0, H), COPY)))
+    e_mz.append(ev(s.activation(mz(1, 0, H), mz(0, 0, H), COPY)))
+    e_mz.append(ev(s.activation(mz(1, H, TL), mz(0, 0, H), COPY)))
 
-    MW = TL + B
-
-    def mz(r):
-        return T.msk[:, r * MW:r * MW + TL]
-    e_low0 = ev(v.memset(T.low0[:], -9e29))
-    e_mz = {p: ev(v.memset(mz(p), 0.0))}
-    e_mz[order[0]] = None
-    need("s", e_mz[p])
-    e_mz[order[0]] = ev(s.activation(mz(order[0]), mz(p), COPY))
-    need("s", e_mz[order[0]])
-    e_mz[order[1]] = ev(s.activation(mz(order[1]), mz(order[0]), COPY))
-    need("v", e_low0)
-    e_low = ev(v.tensor_scalar(T.low[:], T.low0[:], 1e6, None, OP.mult))
-    e_pad = [ev(v.tensor_scalar(T.win[:, 0:PAD], T.low0[:, 0:PAD], 1e6, None, OP.mult)),
-             ev(v.tensor_scalar(T.win[:, PAD + R:WW], T.low0[:, 0:PAD], 1e6, None, OP.mult))]
-
-    need("v", *e_ld)
-    e_c = ev(v.tensor_copy(T.lf[0:16, :], T.lraw[0:16, :]))
-    E, EP, F, D = T.lf[0:16, C1:C2], T.lf[0:16, C2:LW], T.flag[0:16, :], T.spare[0:16, :]
-    need("v", e_c, e_sp)
+    need("v", e_idx)
+    e_c = ev(v.tensor_copy(T.lf[0:16, 0:TC], T.lraw[0:16, 0:TC]))
+    need("t", e_rep, e_c)
+    e_ps = ev(te.matmul(T.ps[:, 0:TC], T.rep[0:16, :], T.lf[0:16, 0:TC], start=True, stop=True))
+    E, EP, F, D = T.lf[0:16, LE:LP], T.lf[0:16, LP:LP + BC], T.flag[0:16, :], T.spare[0:16, :]
+    need("v", *e_end)
+    e_c2 = ev(v.tensor_copy(T.lf[0:16, LE:LP + BC], T.lraw[0:16, LE:LP + BC]))
+    need("v", e_c2)
     e_f = ev(v.tensor_tensor(F, E, EP, OP.is_gt))
-    need("v", e_f)
-    e_1 = ev(v.tensor_tensor(E, E, F, OP.mult))
+    need("v", e_ps)
+    own_list = T.lists[:, p * TC:(p + 1) * TC]
+    e_u = ev(v.tensor_copy(own_list, T.ps[:, 0:TC]))
+    need("v", e_f, e_sp)
     e_2 = ev(v.tensor_tensor(EP, EP, D, OP.subtract))
+    e_1 = ev(v.tensor_tensor(E, E, F, OP.mult))
     need("v", e_2)
     e_3 = ev(v.tensor_tensor(EP, EP, F, OP.mult))
     need("v", e_3)
     e_4 = ev(v.tensor_tensor(EP, EP, D, OP.add))
-    need("t", e_rep, e_c, e_1, e_4)
-    e_ps = ev(te.matmul(T.ps[:, 0:LW], T.rep[0:16, :], T.lf[0:16, :], start=True, stop=True))
-    need("v", e_ps)
-    e_u = ev(v.tensor_copy(lst(p, 0, LW), T.ps[:, 0:LW]))
+    need("t", e_1, e_4)
+    e_ps2 = ev(te.matmul(T.ps2[:, 0:2 * BC], T.rep[0:16, :], T.lf[0:16, LE:LP + BC], start=True, stop=True))
 
-    mask = 0xFFFF
-    for r in others:
-        mask &= topo.mask(core, T.cores[r])
-    ids = []
-    for r in others:
-        rid, pid = topo.addr(T.cores[r], core)
-        ids.append(DstId(rid=rid, pnc=pid))
-    nsent = [0]
+    others = [T.cores[q] for q in range(N) if q != p]
     need("g", e_u)
-    g.remote_dma_fused([RemoteDMATransfer(srcs=[lst(p, 0, LW)], dsts=[lst(p, 0, LW) for r in others], dst_ids=ids,
-                                          dma_engine_mask=mask, remote_sem=T.sem["al%d" % p])], local_sem=T.sem.sent)
-    nsent[0] += bin(mask).count("1")
-    e_mz[order[2]] = ev(g.iota(mz(order[2]), [[0, TL]], 0, 0, allow_small_or_imprecise_dtypes=True))
+    put(others, "al%d" % p, own_list, list_mask(p))
 
-    e_off, e_msk = {}, {}
+    e_off = {}
 
     def clip(r):
         if r == p:
             need("v", e_u)
         else:
-            v.wait_ge(T.sem["al%d" % r], bin(mask).count("1"))
-        e_off[r] = ev(v.tensor_scalar(T.offs[:, r * C1:(r + 1) * C1], lst(r, C0, C1), float(PAD - R * p), float(PAD + R),
-                                      OP.add, OP.min))
+            v.wait_ge(T.sem["al%d" % r], engines(list_mask(r)))
+        e_off[r] = ev(v.tensor_scalar(T.offs[:, r * TC:(r + 1) * TC], T.lists[:, r * TC:(r + 1) * TC],
+                                      float(PAD - R * p), float(PAD + R), OP.add, OP.min))
 
-    def starts(r):
-        need("v", e_mz[r], e_low)
-        if r == p:
-            need("v", e_mz[order[0]])
-        if r == order[0]:
-            need("v", e_mz[order[1]])
-        e_msk[r] = ev(v.tensor_copy(T.msk[:, r * MW:(r + 1) * MW].indirect(lst(r, C2, LW)), T.low[:]))
+    clip(p)
+    need("v", e_ps2)
+    own_cuts = T.cuts[:, 2 * BC * p:2 * BC * (p + 1)]
+    e_cu = ev(v.tensor_copy(own_cuts, T.ps2[:, 0:2 * BC]))
+    need("g", e_cu)
+    put(cut_users(p), "ac%d" % p, own_cuts, cut_mask(p))
 
-    SW = TL + 16
-    e_z = {}
-    for r in range(N):
-        e_z[r] = ev(v.memset(T.scn[:, r * SW + 15:r * SW + 16], 0.0))
+    e_low = low_columns()
+    e_pad = [ev(v.tensor_scalar(T.win[:, 0:PAD], T.low0[:, 0:PAD], 1e6, None, OP.mult)),
+             ev(v.tensor_scalar(T.win[:, PAD + R:WW], T.low0[:, 0:PAD], 1e6, None, OP.mult))]
+    e_z = [ev(v.memset(T.scn[:, k * SW + 15:k * SW + 16], 0.0)) for k in range(2)]
+    need("v", e_cu, e_low, *e_mz)
+    e_mo = mark(0, p)
+    for r in (f1, f2, nr):
+        clip(r)
+    v.wait_ge(T.sem["ac%d" % nr], engines(cut_mask(nr)))
+    e_mn = mark(1, nr)
 
-    CH = [0, 1024, 2048, 3072, 4096]
-    e_g, e_s, e_p = {}, {}, {}
+    e_g = {}
 
-    def gath(name, r, c):
-        a, b = CH[c], CH[c + 1]
+    def gath(name, r, c, ch):
+        a, b = ch[c], ch[c + 1]
         need(name, e_off[r], *e_tab, *e_pad)
         out = T.gat[:, r * TL + a:r * TL + b]
-        src = T.win[:].indirect(T.offs[:, r * C1 + a // 16:r * C1 + b // 16])
+        src = T.win[:].indirect(T.offs[:, r * TC + a // 16:r * TC + b // 16])
         e_g[(r, c)] = ev(v.tensor_copy(out, src) if name == "v" else s.activation(out, src, COPY))
 
-    def scan(r, c):
-        a, b = CH[c], CH[c + 1]
-        need("v", e_g[(r, c)], e_msk[r])
-        o = r * SW + 16
-        init = -9e29
-        if c:
-            need("v", e_s[(r, c - 1)])
-            init = T.scn[:, o + a - 1:o + a]
-        e_s[(r, c)] = ev(v.tensor_tensor_scan(T.scn[:, o + a:o + b], T.msk[:, r * MW + a:r * MW + b],
-                                              T.gat[:, r * TL + a:r * TL + b], init, OP.add, OP.max))
+    gath("s", p, 0, OWN)
+    for r in (f1, f2):
+        gath("s", r, 0, FAR), gath("v", r, 1, FAR)
+        gath("s", r, 2, FAR), gath("v", r, 3, FAR)
+        for c in range(4):
+            need("g", e_g[(r, c)])
+            ap = T.gat[:, r * TL + FAR[c]:r * TL + FAR[c + 1]]
+            send(helper[p], piece(r, c), ap, ap, to_helper)
+    for c in range(3):
+        gath("s", nr, c, NEAR)
+    for c in range(1, len(OWN) - 1):
+        gath("s", p, c, OWN)
+    gath("v", nr, 3, NEAR)
 
-    def bags(r):
-        return T.scn[:, r * SW + 15:(r + 1) * SW].indirect(lst(r, C1, C2))
+    own_last = scan(0, p, OWN[0], OWN[1], [e_g[(p, 0)], e_mo], None)
+    last = None
+    for c in range(4):
+        last = scan(1, nr, NEAR[c], NEAR[c + 1], [e_g[(nr, c)], e_mn], last)
+    need("v", last, e_z[1])
+    out = T.part[:, 0:B]
+    e_p = ev(v.tensor_copy(out, bags(1, nr)))
+    need("g", e_p)
+    send(T.cores[nr], "an", T.landn[:], out, topo.mask(core, T.cores[nr]))
 
-    def extract(r):
-        need("v", e_s[(r, len(CH) - 2)], e_z[r])
-        e_p[r] = ev(v.tensor_copy(T.part[:, r * B:(r + 1) * B], bags(r)))
-
-    def send(r):
-        m = topo.mask(core, T.cores[r])
-        rid, pid = topo.addr(T.cores[r], core)
-        need("g", e_p[r])
-        g.remote_dma(out_ap=T.land[:, p * B:(p + 1) * B], in_ap=T.part[:, r * B:(r + 1) * B], remote_sem=T.sem["ap%d" % p],
-                     local_sem=T.sem.sent, pid=pid, routing_id=rid, dma_engine_mask=m)
-        nsent[0] += bin(m).count("1")
-
-    def landed(r):
-        v.wait_ge(T.sem["ap%d" % r], bin(topo.mask(T.cores[r], core)).count("1"))
-        return T.land[:, r * B:(r + 1) * B]
-
-    f1, f2, nr = order
-    clip(p)
-    starts(p)
-    clip(f1), clip(f2), clip(nr)
-    starts(f1), starts(f2)
-
-    gath("s", p, 0)
-    for r in order:
-        for c in range(3):
-            gath("s", r, c)
-    gath("s", p, 1), gath("s", p, 2)
-
-    gath("v", p, 3), gath("v", f1, 3)
-    scan(p, 0)
-    scan(f1, 0), scan(f1, 1)
-    gath("v", f2, 3)
-    scan(f1, 2), scan(f1, 3), extract(f1), send(f1)
-    starts(nr)
-    scan(f2, 0), scan(f2, 1)
-    gath("v", nr, 3)
-    scan(f2, 2), scan(f2, 3), extract(f2), send(f2)
-    scan(nr, 0), scan(nr, 1), scan(nr, 2), scan(nr, 3), extract(nr), send(nr)
-    e_a = ev(v.tensor_tensor(T.acc[:, 0:B], landed(f1), landed(f2), OP.max))
-    scan(p, 1)
-    need("v", e_a)
-    e_b = ev(v.tensor_tensor(T.acc[:, B:2 * B], landed(nr), T.acc[:, 0:B], OP.max))
-    scan(p, 2), scan(p, 3)
-    need("v", e_b, e_s[(p, 3)], e_z[p])
-    e_y = ev(v.tensor_tensor(T.yt[:], bags(p), T.acc[:, B:2 * B], OP.max))
+    for c in range(1, 4):
+        own_last = scan(0, p, OWN[c], OWN[c + 1], [e_g[(p, c)], e_mo], own_last)
+    v.wait_ge(T.sem.an, engines(topo.mask(T.cores[nr], core)))
+    v.wait_ge(T.sem.af, engines(common(helper[f2], [core, helper[f1]])))
+    e_a = ev(v.tensor_tensor(T.acc[:], T.landn[:], T.landf[:], OP.max))
+    own_last = scan(0, p, OWN[4], OWN[5], [e_g[(p, 4)], e_mo], own_last)
+    need("v", own_last, e_z[0], e_a)
+    e_y = ev(v.tensor_tensor(T.yt[:], bags(0, p), T.acc[:], OP.max))
     need("y", e_y)
     e_o = ev(sy.dma_start(T.y[:], T.yt[:]), 16)
     need("y", e_o)
-    g.wait_ge(T.sem.sent, nsent[0])
-    for e in all_ev:
-        if e[0] not in waited:
-            need("g", e)
+    finish()

@@ -8,20 +8,29 @@ PAD = 16
 WW = R + 2 * PAD
 MW = TL + B
 SW = TL + 16
-NEV = 100
-FAR = [0, 1024, 2048, 3072, 4096]
-NEAR = [0, 1024, 2048, 3072, 4096]
-OWN = [0, 768, 1792, 2816, 3584, 4096]
+NEV = 110
+HEAD = 1024
+PLAN_S = [(3, 0, 1024), (0, 0, 1024), (0, 2048, 3072), (1, 0, 1024), (1, 2048, 3072), (2, 0, 1024), (2, 2048, 3072),
+          (3, 2048, 3072), (3, 3072, 3712), (3, 3712, 4096)]
+PLAN_V = [(0, 1024, 2048), (0, 3072, 4096), (1, 1024, 2048), (1, 3072, 4096), (2, 1024, 2048), (2, 3072, 4096),
+          (3, 1024, 2048)]
+SENDS = [(3, 0, 1024), (0, 0, 1024), (0, 1024, 2048), (0, 2048, 3072), (0, 3072, 4096), (1, 0, 1024), (1, 1024, 2048),
+         (1, 2048, 3072), (1, 3072, 4096), (2, 0, 1024), (2, 1024, 2048), (2, 2048, 3072), (2, 3072, 4096)]
 
 SCRATCH = {
-    "lraw": ("sbuf", [128, TC + 2 * BC], "int32"),
-    "lf": ("sbuf", [128, TC + 2 * BC], "float32"),
+    "lraw": ("sbuf", [128, TC + BC], "int32"),
+    "lf": ("sbuf", [128, TC + 1 + BC], "float32"),
+    "cf": ("sbuf", [128, 2 * BC], "float32"),
     "flag": ("sbuf", [128, BC], "float32"),
+    "spare0": ("sbuf", [128, BC], "float32"),
     "spare": ("sbuf", [128, BC], "float32"),
     "ones": ("sbuf", [128, 128], "float32"),
     "rep": ("sbuf", [128, 128], "float32"),
+    "sh1": ("sbuf", [128, 128], "float32"),
+    "sh2": ("sbuf", [128, 128], "float32"),
     "ps": ("psum", [128, 512], "float32"),
     "ps2": ("psum", [128, 512], "float32"),
+    "ps3": ("psum", [128, 512], "float32"),
     "lists": ("sbuf", [128, N * TC], "uint16"),
     "cuts": ("sbuf", [128, N * 2 * BC], "uint16"),
     "offs": ("sbuf", [128, N * TC], "uint16"),
@@ -38,7 +47,7 @@ SCRATCH = {
     "yt": ("sbuf", [128, B], "bfloat16"),
 }
 SEMAPHORES = (["e%d" % i for i in range(NEV)] + ["al%d" % i for i in range(N)] + ["ac%d" % i for i in range(N)]
-              + ["ag%d" % i for i in range(8)] + ["an", "af", "sent"])
+              + ["ag%d" % i for i in range(len(SENDS))] + ["an", "af", "ao", "sent"])
 
 
 def engines(mask):
@@ -46,16 +55,17 @@ def engines(mask):
 
 
 def rank_program(g, core, T, topo):
-    def helper_of(r):
+    def helpers_of(r):
         c0 = T.cores[r]
         return [c for c in range(WORLD) if topo.host(c) == topo.host(c0) and topo.chip(c) == topo.chip(c0)
-                and topo.die(c) == topo.die(c0) and T.rank_of(c) is None][0]
+                and topo.die(c) == topo.die(c0) and T.rank_of(c) is None][0:2]
 
-    helper = [helper_of(r) for r in range(N)]
-    if core not in T.cores and core not in helper:
+    far_helper = [helpers_of(r)[0] for r in range(N)]
+    near_helper = [helpers_of(r)[1] for r in range(N)]
+    role = "rank" if core in T.cores else "far" if core in far_helper else "near" if core in near_helper else None
+    if role is None:
         return
-    is_rank = core in T.cores
-    p = T.rank_of(core) if is_rank else helper.index(core)
+    p = {"rank": T.cores, "far": far_helper, "near": near_helper}[role].index(core)
 
     def around(q):
         others = [r for r in range(N) if r != q]
@@ -64,6 +74,7 @@ def rank_program(g, core, T, topo):
         return fa + [r for r in others if r not in fa]
 
     f1, f2, nr = around(p)
+    who = [f1, f2, nr, p]
     v, s, te, sy = g.vector, g.scalar, g.tensor, g.sync
     OP, COPY = AluOpType, ActivationFunctionType.Copy
 
@@ -112,15 +123,27 @@ def rank_program(g, core, T, topo):
                      dma_engine_mask=mask)
         nsent[0] += engines(mask)
 
+    def lanes(r, users, dst):
+        away = [d for d in users if topo.chip(d) != topo.chip(T.cores[r]) or topo.host(d) != topo.host(T.cores[r])]
+        out = common(T.cores[r], away)
+        return out if dst in away else topo.mask(T.cores[r], dst) & ~out
+
+    def give(r, users, sem, ap):
+        for m in sorted(set(lanes(r, users, d) for d in users)):
+            put([d for d in users if lanes(r, users, d) == m], sem, ap, m)
+
     def cut_users(r):
         a, b, c = around(r)
-        return [T.cores[c], helper[a], helper[b]]
+        return [near_helper[c], near_helper[r], far_helper[a], far_helper[b]]
 
     def cut_mask(r):
-        return common(T.cores[r], cut_users(r))
+        return lanes(r, cut_users(r), core)
+
+    def list_users(r):
+        return [T.cores[q] for q in range(N) if q != r]
 
     def list_mask(r):
-        return common(T.cores[r], [T.cores[q] for q in range(N) if q != r])
+        return lanes(r, list_users(r), core)
 
     def ends(r):
         return T.cuts[:, 2 * BC * r:2 * BC * r + BC]
@@ -139,10 +162,10 @@ def rank_program(g, core, T, topo):
         o = k * SW + 16
         init = -9e29
         if a:
-            need("v", last)
+            need("v", *last)
             init = T.scn[:, o + a - 1:o + a]
-        return ev(v.tensor_tensor_scan(T.scn[:, o + a:o + b], mz(k, a, b), T.gat[:, r * TL + a:r * TL + b], init,
-                                       OP.add, OP.max))
+        return [ev(v.tensor_tensor_scan(T.scn[:, o + a:o + b], mz(k, a, b), T.gat[:, r * TL + a:r * TL + b], init,
+                                        OP.add, OP.max))]
 
     def bags(k, r):
         return T.scn[:, k * SW + 15:(k + 1) * SW].indirect(ends(r))
@@ -152,14 +175,22 @@ def rank_program(g, core, T, topo):
         need("v", e)
         return ev(v.tensor_scalar(T.low[:], T.low0[:], 1e6, None, OP.mult))
 
-    def piece(r, c):
-        return "ag%d" % (4 * [f1, f2].index(r) + c)
+    def helper_for(l):
+        return (far_helper if l < 2 else near_helper)[p]
 
-    to_helper = topo.mask(T.cores[p], helper[p])
+    def piece_mask(l):
+        return topo.mask(T.cores[p], helper_for(l))
 
-    if not is_rank:
-        rank_core = T.cores[p]
-        mate = helper[nr]
+    def scan_pieces(k, l, e_k):
+        last = []
+        for i, (m, a, b) in enumerate(SENDS):
+            if m == l:
+                v.wait_ge(T.sem["ag%d" % i], engines(piece_mask(l)))
+                last = scan(k, who[l], a, b, [e_k], last)
+        return last
+
+    if role == "far":
+        mate = far_helper[nr]
         pm = common(core, [T.cores[f2], mate])
         mate_pm = common(mate, [T.cores[f1], core])
         e_z = [ev(v.memset(T.scn[:, k * SW + 15:k * SW + 16], 0.0)) for k in range(2)]
@@ -171,11 +202,8 @@ def rank_program(g, core, T, topo):
             need("v", e_m[k], e_low)
             e_k.append(mark(k, r))
         for k, r in enumerate((f1, f2)):
-            last = None
-            for c in range(len(FAR) - 1):
-                v.wait_ge(T.sem[piece(r, c)], engines(to_helper))
-                last = scan(k, r, FAR[c], FAR[c + 1], [e_k[k]], last)
-            need("v", last, e_z[k])
+            last = scan_pieces(k, k, e_k[k])
+            need("v", *last, e_z[k])
             out = T.part[:, k * B:(k + 1) * B]
             if k == 0:
                 e_p = ev(v.tensor_copy(out, bags(k, r)))
@@ -189,122 +217,132 @@ def rank_program(g, core, T, topo):
         finish()
         return
 
-    LE, LP = TC, TC + BC
-    e_m0 = ev(v.memset(T.lraw[0:16, LP:LP + BC], 0))
-    e_ones = ev(v.memset(T.ones[0:16, :], 1.0))
-    e_idx = ev(sy.dma_start(T.lraw[0:16, 0:TC], T.idx[:]), 16)
-    e_end = [ev(sy.dma_start(T.lraw[0:16, LE:LP], T.end[:]), 16)]
-    e_tab = [ev(sy.dma_start(T.win[:, PAD:PAD + R // 2], T.tab[:, 0:R // 2]), 16)]
-    need("s", e_m0)
-    e_end.append(ev(s.dma_start(T.lraw[1:16, LP:LP + BC], T.end[0:15, :]), 16))
-    e_end.append(ev(s.dma_start(T.lraw[0:1, LP + 1:LP + BC], T.end[15:16, 0:BC - 1]), 16))
-    e_tab.append(ev(s.dma_start(T.win[:, PAD + R // 2:PAD + R], T.tab[:, R // 2:R]), 16))
+    if role == "near":
+        pm = common(core, [T.cores[p], T.cores[nr]])
+        e_z = ev(v.memset(T.scn[:, SW + 15:SW + 16], 0.0))
+        e_low = low_columns()
+        e_m = [ev(v.memset(mz(0, 0, HEAD), 0.0)), ev(v.memset(mz(1), 0.0))]
+        e_k = []
+        for k, r in enumerate((p, nr)):
+            v.wait_ge(T.sem["ac%d" % r], engines(cut_mask(r)))
+            need("v", e_m[k], e_low)
+            e_k.append(mark(k, r))
+        last = scan_pieces(0, 3, e_k[0])
+        need("g", *last)
+        ap = T.scn[:, 16:16 + HEAD]
+        send(T.cores[p], "ao", ap, ap, pm)
+        last = scan_pieces(1, 2, e_k[1])
+        need("v", *last, e_z)
+        out = T.part[:, B:2 * B]
+        e_p = ev(v.tensor_copy(out, bags(1, nr)))
+        need("g", e_p)
+        send(T.cores[nr], "an", T.landn[:], out, pm)
+        finish()
+        return
 
+    LE = TC + 1
+    e_idx = ev(sy.dma_start(T.lraw[0:16, 0:TC], T.idx[:]), 16)
+    e_end = ev(s.dma_start(T.lraw[0:16, TC:TC + BC], T.end[:]), 16)
+    e_tab = ev(sy.dma_start(T.win[:, PAD:PAD + R], T.tab[:]), 16)
+
+    e_ones = ev(v.memset(T.ones[0:16, :], 1.0))
+    e_z0 = ev(v.memset(T.lf[0:16, TC:TC + 1], 0.0))
     need("g", e_ones)
     e_rep = ev(g.affine_select(T.rep[0:16, :], T.ones[0:16, :], [[0, 8], [1, 16]], OP.is_equal, 0.0, 0, -1))
-    e_sp = ev(g.iota(T.spare[0:16, :], [[16, BC]], TL, 1, allow_small_or_imprecise_dtypes=True))
-    H = TL // 2
-    e_mz = [ev(v.memset(mz(0, 0, H), 0.0))]
-    need("s", e_mz[0])
-    e_mz.append(ev(s.activation(mz(0, H, TL), mz(0, 0, H), COPY)))
-    e_mz.append(ev(s.activation(mz(1, 0, H), mz(0, 0, H), COPY)))
-    e_mz.append(ev(s.activation(mz(1, H, TL), mz(0, 0, H), COPY)))
+    e_sp = ev(g.iota(T.spare0[0:16, :], [[16, BC]], TL, 1, allow_small_or_imprecise_dtypes=True))
+    e_s1 = ev(g.affine_select(T.sh1[0:16, :], T.ones[0:16, :], [[0, 8], [1, 16]], OP.is_equal, 0.0, -1, -1))
+    e_s2 = ev(g.affine_select(T.sh2[0:16, :], T.ones[0:16, :], [[0, 8], [1, 16]], OP.is_equal, 0.0, 15, -1))
+    e_low0 = ev(v.memset(T.low0[:], -9e29))
+    need("v", e_low0)
+    e_pad = [ev(v.tensor_scalar(T.win[:, 0:PAD], T.low0[:, 0:PAD], 1e6, None, OP.mult)),
+             ev(v.tensor_scalar(T.win[:, PAD + R:WW], T.low0[:, 0:PAD], 1e6, None, OP.mult))]
 
     need("v", e_idx)
     e_c = ev(v.tensor_copy(T.lf[0:16, 0:TC], T.lraw[0:16, 0:TC]))
+    need("v", e_end)
+    e_c2 = ev(v.tensor_copy(T.lf[0:16, LE:LE + BC], T.lraw[0:16, TC:TC + BC]))
     need("t", e_rep, e_c)
     e_ps = ev(te.matmul(T.ps[:, 0:TC], T.rep[0:16, :], T.lf[0:16, 0:TC], start=True, stop=True))
-    E, EP, F, D = T.lf[0:16, LE:LP], T.lf[0:16, LP:LP + BC], T.flag[0:16, :], T.spare[0:16, :]
-    need("v", *e_end)
-    e_c2 = ev(v.tensor_copy(T.lf[0:16, LE:LP + BC], T.lraw[0:16, LE:LP + BC]))
-    need("v", e_c2)
-    e_f = ev(v.tensor_tensor(F, E, EP, OP.is_gt))
+    need("t", e_sp)
+    e_ps3 = ev(te.matmul(T.ps3[:, 0:BC], T.rep[0:16, :], T.spare0[0:16, :], start=True, stop=True))
+    need("t", e_c2, e_s1, e_s2, e_z0)
+    E, EP = T.lf[0:16, LE:LE + BC], T.lf[0:16, TC:TC + BC]
+    e_ps2 = [ev(te.matmul(T.ps2[:, 0:BC], T.rep[0:16, :], E, start=True, stop=True))]
+    te.matmul(T.ps2[:, BC:2 * BC], T.sh1[0:16, :], E, start=True, stop=False)
+    e_ps2.append(ev(te.matmul(T.ps2[:, BC:2 * BC], T.sh2[0:16, :], EP, start=False, stop=True)))
     need("v", e_ps)
     own_list = T.lists[:, p * TC:(p + 1) * TC]
     e_u = ev(v.tensor_copy(own_list, T.ps[:, 0:TC]))
-    need("v", e_f, e_sp)
-    e_2 = ev(v.tensor_tensor(EP, EP, D, OP.subtract))
-    e_1 = ev(v.tensor_tensor(E, E, F, OP.mult))
-    need("v", e_2)
-    e_3 = ev(v.tensor_tensor(EP, EP, F, OP.mult))
-    need("v", e_3)
-    e_4 = ev(v.tensor_tensor(EP, EP, D, OP.add))
-    need("t", e_1, e_4)
-    e_ps2 = ev(te.matmul(T.ps2[:, 0:2 * BC], T.rep[0:16, :], T.lf[0:16, LE:LP + BC], start=True, stop=True))
-
-    others = [T.cores[q] for q in range(N) if q != p]
     need("g", e_u)
-    put(others, "al%d" % p, own_list, list_mask(p))
+    give(p, list_users(p), "al%d" % p, own_list)
+
+    F, D, CE, CS = T.flag[:], T.spare[:], T.cf[:, 0:BC], T.cf[:, BC:2 * BC]
+    need("v", e_ps3)
+    e_d = ev(v.tensor_copy(D, T.ps3[:, 0:BC]))
+    need("v", *e_ps2)
+    e_cf = ev(v.tensor_copy(T.cf[:], T.ps2[:, 0:2 * BC]))
+    need("v", e_cf, e_d)
+    e_f = ev(v.tensor_tensor(F, CE, CS, OP.is_gt))
+    e_2 = ev(v.tensor_tensor(CS, CS, D, OP.subtract))
+    need("v", e_f, e_2)
+    e_1 = ev(v.tensor_tensor(CE, CE, F, OP.mult))
+    e_3 = ev(v.tensor_tensor(CS, CS, F, OP.mult))
+    need("v", e_1, e_3)
+    e_4 = ev(v.tensor_tensor(CS, CS, D, OP.add))
+    need("v", e_4)
+    own_cuts = T.cuts[:, 2 * BC * p:2 * BC * (p + 1)]
+    e_cu = ev(v.tensor_copy(own_cuts, T.cf[:]))
+    need("g", e_cu)
+    give(p, cut_users(p), "ac%d" % p, own_cuts)
 
     e_off = {}
 
-    def clip(r):
+    def clip(l):
+        r = who[l]
         if r == p:
             need("v", e_u)
         else:
             v.wait_ge(T.sem["al%d" % r], engines(list_mask(r)))
-        e_off[r] = ev(v.tensor_scalar(T.offs[:, r * TC:(r + 1) * TC], T.lists[:, r * TC:(r + 1) * TC],
+        e_off[l] = ev(v.tensor_scalar(T.offs[:, r * TC:(r + 1) * TC], T.lists[:, r * TC:(r + 1) * TC],
                                       float(PAD - R * p), float(PAD + R), OP.add, OP.min))
 
-    clip(p)
-    need("v", e_ps2)
-    own_cuts = T.cuts[:, 2 * BC * p:2 * BC * (p + 1)]
-    e_cu = ev(v.tensor_copy(own_cuts, T.ps2[:, 0:2 * BC]))
-    need("g", e_cu)
-    put(cut_users(p), "ac%d" % p, own_cuts, cut_mask(p))
-
-    e_low = low_columns()
-    e_pad = [ev(v.tensor_scalar(T.win[:, 0:PAD], T.low0[:, 0:PAD], 1e6, None, OP.mult)),
-             ev(v.tensor_scalar(T.win[:, PAD + R:WW], T.low0[:, 0:PAD], 1e6, None, OP.mult))]
-    e_z = [ev(v.memset(T.scn[:, k * SW + 15:k * SW + 16], 0.0)) for k in range(2)]
-    need("v", e_cu, e_low, *e_mz)
+    clip(3)
+    e_low = ev(v.tensor_scalar(T.low[:], T.low0[:], 1e6, None, OP.mult))
+    e_z = ev(v.memset(T.scn[:, 15:16], 0.0))
+    e_mz = ev(v.memset(mz(0, HEAD, TL), 0.0))
+    need("v", e_cu, e_low, e_mz)
     e_mo = mark(0, p)
-    for r in (f1, f2, nr):
-        clip(r)
-    v.wait_ge(T.sem["ac%d" % nr], engines(cut_mask(nr)))
-    e_mn = mark(1, nr)
+    for l in range(3):
+        clip(l)
 
     e_g = {}
 
-    def gath(name, r, c, ch):
-        a, b = ch[c], ch[c + 1]
-        need(name, e_off[r], *e_tab, *e_pad)
+    def gath(name, l, a, b):
+        r = who[l]
+        need(name, e_off[l], e_tab, *e_pad)
         out = T.gat[:, r * TL + a:r * TL + b]
         src = T.win[:].indirect(T.offs[:, r * TC + a // 16:r * TC + b // 16])
-        e_g[(r, c)] = ev(v.tensor_copy(out, src) if name == "v" else s.activation(out, src, COPY))
+        e_g[(l, a, b)] = ev(v.tensor_copy(out, src) if name == "v" else s.activation(out, src, COPY))
 
-    gath("s", p, 0, OWN)
-    for r in (f1, f2):
-        gath("s", r, 0, FAR), gath("v", r, 1, FAR)
-        gath("s", r, 2, FAR), gath("v", r, 3, FAR)
-        for c in range(4):
-            need("g", e_g[(r, c)])
-            ap = T.gat[:, r * TL + FAR[c]:r * TL + FAR[c + 1]]
-            send(helper[p], piece(r, c), ap, ap, to_helper)
-    for c in range(3):
-        gath("s", nr, c, NEAR)
-    for c in range(1, len(OWN) - 1):
-        gath("s", p, c, OWN)
-    gath("v", nr, 3, NEAR)
+    for x in PLAN_S:
+        gath("s", *x)
+    for x in PLAN_V:
+        gath("v", *x)
+    for i, (l, a, b) in enumerate(SENDS):
+        need("g", e_g[(l, a, b)])
+        ap = T.gat[:, who[l] * TL + a:who[l] * TL + b]
+        send(helper_for(l), "ag%d" % i, ap, ap, piece_mask(l))
 
-    own_last = scan(0, p, OWN[0], OWN[1], [e_g[(p, 0)], e_mo], None)
-    last = None
-    for c in range(4):
-        last = scan(1, nr, NEAR[c], NEAR[c + 1], [e_g[(nr, c)], e_mn], last)
-    need("v", last, e_z[1])
-    out = T.part[:, 0:B]
-    e_p = ev(v.tensor_copy(out, bags(1, nr)))
-    need("g", e_p)
-    send(T.cores[nr], "an", T.landn[:], out, topo.mask(core, T.cores[nr]))
-
-    for c in range(1, 4):
-        own_last = scan(0, p, OWN[c], OWN[c + 1], [e_g[(p, c)], e_mo], own_last)
-    v.wait_ge(T.sem.an, engines(topo.mask(T.cores[nr], core)))
-    v.wait_ge(T.sem.af, engines(common(helper[f2], [core, helper[f1]])))
-    e_a = ev(v.tensor_tensor(T.acc[:], T.landn[:], T.landf[:], OP.max))
-    own_last = scan(0, p, OWN[4], OWN[5], [e_g[(p, 4)], e_mo], own_last)
-    need("v", own_last, e_z[0], e_a)
-    e_y = ev(v.tensor_tensor(T.yt[:], bags(0, p), T.acc[:], OP.max))
+    v.wait_ge(T.sem.ao, engines(common(near_helper[p], [core, T.cores[nr]])))
+    last = []
+    for a, b in sorted([(a, b) for (l, a, b) in PLAN_S + PLAN_V if l == 3 and a >= HEAD]):
+        last = scan(0, p, a, b, [e_g[(3, a, b)], e_mo], last)
+    v.wait_ge(T.sem.af, engines(common(far_helper[f2], [core, far_helper[f1]])))
+    need("v", *last, e_z)
+    e_a = ev(v.tensor_tensor(T.acc[:], bags(0, p), T.landf[:], OP.max))
+    need("v", e_a)
+    v.wait_ge(T.sem.an, engines(common(near_helper[nr], [core, T.cores[nr]])))
+    e_y = ev(v.tensor_tensor(T.yt[:], T.acc[:], T.landn[:], OP.max))
     need("y", e_y)
     e_o = ev(sy.dma_start(T.y[:], T.yt[:]), 16)
     need("y", e_o)

@@ -6,20 +6,27 @@ WORLD = 256
 TC, BC = TL // 16, B // 16
 PAD = 16
 WW = R + 2 * PAD
+CA = 14336
+CB = R - CA
 MW = TL + B
 SW = TL + 16
-NEV = 110
-HEAD = 1024
-PLAN_S = [(3, 0, 1024), (0, 0, 1024), (0, 2048, 3072), (1, 0, 1024), (1, 2048, 3072), (2, 0, 1024), (2, 2048, 3072),
-          (3, 2048, 3072), (3, 3072, 3712), (3, 3712, 4096)]
-PLAN_V = [(0, 1024, 2048), (0, 3072, 4096), (1, 1024, 2048), (1, 3072, 4096), (2, 1024, 2048), (2, 3072, 4096),
-          (3, 1024, 2048)]
-SENDS = [(3, 0, 1024), (0, 0, 1024), (0, 1024, 2048), (0, 2048, 3072), (0, 3072, 4096), (1, 0, 1024), (1, 1024, 2048),
-         (1, 2048, 3072), (1, 3072, 4096), (2, 0, 1024), (2, 1024, 2048), (2, 2048, 3072), (2, 3072, 4096)]
+NEV = 100
+HEAD = 2560
+HC = HEAD // 16
+EARLY_S, EARLY_V = (0, 1312), (1312, 2560)
+OWN_S = 1280
+PUSH = 0
+PLAN_S = [(0, 0, 1024), (0, 2048, 3072), (1, 0, 1024), (1, 2048, 3072), (2, 0, 768), (2, 1536, 2304), (2, 3072, 3584),
+          (3, 2560, 3328), (3, 3328, 3712), (3, 3904, 4096)]
+PLAN_V = [(0, 1024, 2048), (0, 3072, 4096), (1, 1024, 2048), (1, 3072, 4096), (2, 768, 1536), (2, 2304, 3072), (2, 3584, 4096),
+          (3, 3712, 3904)]
+SENDS = [(0, 0, 2048), (0, 2048, 4096), (1, 0, 2048), (1, 2048, 4096), (2, 0, 1536), (2, 1536, 3072), (2, 3072, 4096)]
 
 SCRATCH = {
     "lraw": ("sbuf", [128, TC + BC], "int32"),
     "lf": ("sbuf", [128, TC + 1 + BC], "float32"),
+    "fa": ("sbuf", [128, HC], "float32"),
+    "fb": ("sbuf", [128, HC], "float32"),
     "cf": ("sbuf", [128, 2 * BC], "float32"),
     "flag": ("sbuf", [128, BC], "float32"),
     "spare0": ("sbuf", [128, BC], "float32"),
@@ -34,6 +41,8 @@ SCRATCH = {
     "lists": ("sbuf", [128, N * TC], "uint16"),
     "cuts": ("sbuf", [128, N * 2 * BC], "uint16"),
     "offs": ("sbuf", [128, N * TC], "uint16"),
+    "offa": ("sbuf", [128, HC], "uint16"),
+    "offb": ("sbuf", [128, HC], "uint16"),
     "low0": ("sbuf", [128, B], "bfloat16"),
     "low": ("sbuf", [128, B], "bfloat16"),
     "win": ("sbuf", [128, WW], "bfloat16"),
@@ -41,13 +50,16 @@ SCRATCH = {
     "gat": ("sbuf", [128, N * TL], "bfloat16"),
     "scn": ("sbuf", [128, 2 * SW], "bfloat16"),
     "part": ("sbuf", [128, 2 * B], "bfloat16"),
+    "pick": ("sbuf", [128, B], "bfloat16"),
     "landn": ("sbuf", [128, B], "bfloat16"),
     "landf": ("sbuf", [128, B], "bfloat16"),
+    "lando": ("sbuf", [128, B], "bfloat16"),
+    "pre": ("sbuf", [128, B], "bfloat16"),
     "acc": ("sbuf", [128, B], "bfloat16"),
     "yt": ("sbuf", [128, B], "bfloat16"),
 }
 SEMAPHORES = (["e%d" % i for i in range(NEV)] + ["al%d" % i for i in range(N)] + ["ac%d" % i for i in range(N)]
-              + ["ag%d" % i for i in range(len(SENDS))] + ["an", "af", "ao", "sent"])
+              + ["ag%d" % i for i in range(len(SENDS))] + ["an", "af", "ao", "am", "ob", "ow", "sent"])
 
 
 def engines(mask):
@@ -58,14 +70,17 @@ def rank_program(g, core, T, topo):
     def helpers_of(r):
         c0 = T.cores[r]
         return [c for c in range(WORLD) if topo.host(c) == topo.host(c0) and topo.chip(c) == topo.chip(c0)
-                and topo.die(c) == topo.die(c0) and T.rank_of(c) is None][0:2]
+                and topo.die(c) == topo.die(c0) and T.rank_of(c) is None][0:3]
 
     far_helper = [helpers_of(r)[0] for r in range(N)]
     near_helper = [helpers_of(r)[1] for r in range(N)]
-    role = "rank" if core in T.cores else "far" if core in far_helper else "near" if core in near_helper else None
-    if role is None:
+    own_helper = [helpers_of(r)[2] for r in range(N)]
+    crews = {"rank": T.cores, "far": far_helper, "near": near_helper, "own": own_helper}
+    mine = [k for k in crews if core in crews[k]]
+    if not mine:
         return
-    p = {"rank": T.cores, "far": far_helper, "near": near_helper}[role].index(core)
+    role = mine[0]
+    p = crews[role].index(core)
 
     def around(q):
         others = [r for r in range(N) if r != q]
@@ -134,19 +149,21 @@ def rank_program(g, core, T, topo):
 
     def cut_users(r):
         a, b, c = around(r)
-        return [near_helper[c], near_helper[r], far_helper[a], far_helper[b]]
-
-    def cut_mask(r):
-        return lanes(r, cut_users(r), core)
+        return [near_helper[r], near_helper[c], own_helper[r], far_helper[a], far_helper[b]]
 
     def list_users(r):
         return [T.cores[q] for q in range(N) if q != r]
 
-    def list_mask(r):
-        return lanes(r, list_users(r), core)
+    def cuts_here(r):
+        for q in (v, s):
+            q.wait_ge(T.sem["ac%d" % r], engines(lanes(r, cut_users(r), core)))
 
-    def ends(r):
-        return T.cuts[:, 2 * BC * r:2 * BC * r + BC]
+    H = BC // 2
+    HB = B // 2
+
+    def ends(r, h):
+        o = 2 * BC * r + h * H
+        return T.cuts[:, o:o + H]
 
     def starts(r):
         return T.cuts[:, 2 * BC * r + BC:2 * BC * (r + 1)]
@@ -157,7 +174,7 @@ def rank_program(g, core, T, topo):
     def mark(k, r):
         return ev(v.tensor_copy(T.msk[:, k * MW:(k + 1) * MW].indirect(starts(r)), T.low[:]))
 
-    def scan(k, r, a, b, deps, last):
+    def scan_of(k, r, a, b, deps, last):
         need("v", *deps)
         o = k * SW + 16
         init = -9e29
@@ -167,8 +184,22 @@ def rank_program(g, core, T, topo):
         return [ev(v.tensor_tensor_scan(T.scn[:, o + a:o + b], mz(k, a, b), T.gat[:, r * TL + a:r * TL + b], init,
                                         OP.add, OP.max))]
 
-    def bags(k, r):
-        return T.scn[:, k * SW + 15:(k + 1) * SW].indirect(ends(r))
+    def bags(k, r, h):
+        return T.scn[:, k * SW + 15:(k + 1) * SW].indirect(ends(r, h))
+
+    def half(t, h, k=0):
+        return t[:, k * B + h * HB:k * B + (h + 1) * HB]
+
+    def picks(k, r, deps, out_k, out, other=None):
+        need("v", *deps)
+        need("s", *deps)
+        if other is None:
+            return [ev(v.tensor_copy(half(out, 0, out_k), bags(k, r, 0))),
+                    ev(s.activation(half(out, 1, out_k), bags(k, r, 1), COPY))]
+        e_s = ev(s.activation(half(T.pick, 1), bags(k, r, 1), COPY))
+        e = [ev(v.tensor_tensor(half(out, 0, out_k), bags(k, r, 0), half(other, 0), OP.max))]
+        need("v", e_s)
+        return e + [ev(v.tensor_tensor(half(out, 1, out_k), half(T.pick, 1), half(other, 1), OP.max))]
 
     def low_columns():
         e = ev(v.memset(T.low0[:], -9e29))
@@ -186,8 +217,14 @@ def rank_program(g, core, T, topo):
         for i, (m, a, b) in enumerate(SENDS):
             if m == l:
                 v.wait_ge(T.sem["ag%d" % i], engines(piece_mask(l)))
-                last = scan(k, who[l], a, b, [e_k], last)
+                last = scan_of(k, who[l], a, b, [e_k], last)
         return last
+
+    own_mask = topo.mask(T.cores[p], own_helper[p])
+    back_mask = topo.mask(own_helper[p], T.cores[p])
+
+    def near_mask(q):
+        return common(near_helper[q], [T.cores[q], T.cores[around(q)[2]]])
 
     if role == "far":
         mate = far_helper[nr]
@@ -198,52 +235,75 @@ def rank_program(g, core, T, topo):
         e_m = [ev(v.memset(mz(k), 0.0)) for k in range(2)]
         e_k = []
         for k, r in enumerate((f1, f2)):
-            v.wait_ge(T.sem["ac%d" % r], engines(cut_mask(r)))
+            cuts_here(r)
             need("v", e_m[k], e_low)
             e_k.append(mark(k, r))
         for k, r in enumerate((f1, f2)):
             last = scan_pieces(k, k, e_k[k])
-            need("v", *last, e_z[k])
             out = T.part[:, k * B:(k + 1) * B]
             if k == 0:
-                e_p = ev(v.tensor_copy(out, bags(k, r)))
-                need("g", e_p)
+                e_p = picks(k, r, last + [e_z[k]], k, T.part)
+                need("g", *e_p)
                 send(mate, "an", T.landn[:], out, pm)
             else:
                 v.wait_ge(T.sem.an, engines(mate_pm))
-                e_p = ev(v.tensor_tensor(out, bags(k, r), T.landn[:], OP.max))
-                need("g", e_p)
+                e_p = picks(k, r, last + [e_z[k]], k, T.part, T.landn)
+                need("g", *e_p)
                 send(T.cores[r], "af", T.landf[:], out, pm)
         finish()
         return
 
     if role == "near":
-        pm = common(core, [T.cores[p], T.cores[nr]])
-        e_z = ev(v.memset(T.scn[:, SW + 15:SW + 16], 0.0))
+        e_z = ev(v.memset(T.scn[:, 15:16], 0.0))
         e_low = low_columns()
-        e_m = [ev(v.memset(mz(0, 0, HEAD), 0.0)), ev(v.memset(mz(1), 0.0))]
-        e_k = []
-        for k, r in enumerate((p, nr)):
-            v.wait_ge(T.sem["ac%d" % r], engines(cut_mask(r)))
-            need("v", e_m[k], e_low)
-            e_k.append(mark(k, r))
-        last = scan_pieces(0, 3, e_k[0])
-        need("g", *last)
-        ap = T.scn[:, 16:16 + HEAD]
-        send(T.cores[p], "ao", ap, ap, pm)
-        last = scan_pieces(1, 2, e_k[1])
-        need("v", *last, e_z)
-        out = T.part[:, B:2 * B]
-        e_p = ev(v.tensor_copy(out, bags(1, nr)))
-        need("g", e_p)
-        send(T.cores[nr], "an", T.landn[:], out, pm)
+        e_m = [ev(v.memset(mz(k), 0.0)) for k in range(2)]
+        cuts_here(p)
+        need("v", *e_m, e_low)
+        e_k = mark(1, p)
+        need("g", e_k)
+        send(T.cores[p], "am", mz(0), mz(1), near_mask(p))
+        cuts_here(nr)
+        last = scan_pieces(0, 2, mark(0, nr))
+        e_p = picks(0, nr, last + [e_z], 0, T.part)
+        need("g", *e_p)
+        send(T.cores[nr], "an", T.landn[:], T.part[:, 0:B], near_mask(p))
+        finish()
+        return
+
+    if role == "own":
+        e_z = ev(v.memset(T.scn[:, 15:16], 0.0))
+        e_low = low_columns()
+        need("v", e_low)
+        e_pad = [ev(v.tensor_copy(T.win[:, 0:PAD], T.low[:, 0:PAD])),
+                 ev(v.tensor_copy(T.win[:, PAD + CB:CB + 2 * PAD], T.low[:, 0:PAD]))]
+        e_m = ev(v.memset(mz(0), 0.0))
+        need("s", e_low)
+        o = p * TL
+        e_fill = [ev(s.activation(T.gat[:, o + a:o + a + B], T.low[:], COPY)) for a in range(HEAD, TL, B)]
+        cuts_here(p)
+        need("v", e_m)
+        e_k = mark(0, p)
+        win = T.win[:, 0:CB + 2 * PAD]
+        for q, name in ((v, "v"), (s, "s")):
+            q.wait_ge(T.sem.ob, engines(own_mask))
+            q.wait_ge(T.sem.ow, engines(own_mask))
+            need(name, *e_pad)
+        e_s = ev(s.activation(T.gat[:, o:o + OWN_S], win.indirect(T.offb[:, 0:OWN_S // 16]), COPY))
+        e_v = ev(v.tensor_copy(T.gat[:, o + OWN_S:o + HEAD], win.indirect(T.offb[:, OWN_S // 16:HC])))
+        last = scan_of(0, p, 0, OWN_S, [e_k, e_s], [])
+        last = scan_of(0, p, OWN_S, HEAD, [e_v], last)
+        last = scan_of(0, p, HEAD, TL, e_fill, last)
+        e_p = picks(0, p, last + [e_z], 0, T.part)
+        need("g", *e_p)
+        send(T.cores[p], "ao", T.lando[:], T.part[:, 0:B], back_mask)
         finish()
         return
 
     LE = TC + 1
     e_idx = ev(sy.dma_start(T.lraw[0:16, 0:TC], T.idx[:]), 16)
     e_end = ev(s.dma_start(T.lraw[0:16, TC:TC + BC], T.end[:]), 16)
-    e_tab = ev(sy.dma_start(T.win[:, PAD:PAD + R], T.tab[:]), 16)
+    e_ta = ev(sy.dma_start(T.win[:, PAD:PAD + CA], T.tab[:, 0:CA]), 16)
+    e_tb = ev(sy.dma_start(T.win[:, PAD + CA:PAD + R], T.tab[:, CA:R]), 16)
 
     e_ones = ev(v.memset(T.ones[0:16, :], 1.0))
     e_z0 = ev(v.memset(T.lf[0:16, TC:TC + 1], 0.0))
@@ -252,10 +312,11 @@ def rank_program(g, core, T, topo):
     e_sp = ev(g.iota(T.spare0[0:16, :], [[16, BC]], TL, 1, allow_small_or_imprecise_dtypes=True))
     e_s1 = ev(g.affine_select(T.sh1[0:16, :], T.ones[0:16, :], [[0, 8], [1, 16]], OP.is_equal, 0.0, -1, -1))
     e_s2 = ev(g.affine_select(T.sh2[0:16, :], T.ones[0:16, :], [[0, 8], [1, 16]], OP.is_equal, 0.0, 15, -1))
-    e_low0 = ev(v.memset(T.low0[:], -9e29))
+    e_low0 = ev(v.memset(T.low0[:, 0:PAD], -9e29))
     need("v", e_low0)
     e_pad = [ev(v.tensor_scalar(T.win[:, 0:PAD], T.low0[:, 0:PAD], 1e6, None, OP.mult)),
              ev(v.tensor_scalar(T.win[:, PAD + R:WW], T.low0[:, 0:PAD], 1e6, None, OP.mult))]
+    e_z = ev(v.memset(T.scn[:, 15:16], 0.0))
 
     need("v", e_idx)
     e_c = ev(v.tensor_copy(T.lf[0:16, 0:TC], T.lraw[0:16, 0:TC]))
@@ -273,14 +334,27 @@ def rank_program(g, core, T, topo):
     need("v", e_ps)
     own_list = T.lists[:, p * TC:(p + 1) * TC]
     e_u = ev(v.tensor_copy(own_list, T.ps[:, 0:TC]))
-    need("g", e_u)
-    give(p, list_users(p), "al%d" % p, own_list)
+    need("v", e_u)
+    for q in (f1, f2, nr):
+        out = T.lists[:, q * TC:(q + 1) * TC]
+        e_l = ev(v.tensor_scalar(out, own_list, float(PAD - R * q), float(PAD + R), OP.add, OP.min))
+        need("g", e_l)
+        send(T.cores[q], "al%d" % p, T.offs[:, p * TC:(p + 1) * TC], out, lanes(p, list_users(p), T.cores[q]))
 
-    F, D, CE, CS = T.flag[:], T.spare[:], T.cf[:, 0:BC], T.cf[:, BC:2 * BC]
+    c0 = float(PAD - R * p)
+    raw = T.ps[:, 0:HC]
+    e_fa = ev(v.tensor_scalar(T.fa[:], raw, c0, float(PAD + CA), OP.add, OP.is_lt))
+    e_fb = ev(v.tensor_scalar(T.fb[:], raw, c0, None, OP.add))
     need("v", e_ps3)
-    e_d = ev(v.tensor_copy(D, T.ps3[:, 0:BC]))
+    e_d = ev(v.tensor_copy(T.spare[:], T.ps3[:, 0:BC]))
+    need("v", e_fa, e_fb)
+    e_fm = ev(v.tensor_tensor(T.fa[:], T.fa[:], T.fb[:], OP.mult))
     need("v", *e_ps2)
     e_cf = ev(v.tensor_copy(T.cf[:], T.ps2[:, 0:2 * BC]))
+    need("v", e_fm)
+    e_oa = ev(v.tensor_copy(T.offa[:], T.fa[:]))
+
+    F, D, CE, CS = T.flag[:], T.spare[:], T.cf[:, 0:BC], T.cf[:, BC:2 * BC]
     need("v", e_cf, e_d)
     e_f = ev(v.tensor_tensor(F, CE, CS, OP.is_gt))
     e_2 = ev(v.tensor_tensor(CS, CS, D, OP.subtract))
@@ -295,54 +369,58 @@ def rank_program(g, core, T, topo):
     need("g", e_cu)
     give(p, cut_users(p), "ac%d" % p, own_cuts)
 
-    e_off = {}
+    e_ob = ev(v.tensor_scalar(T.offb[:], raw, c0 - CA, float(PAD + CB), OP.add, OP.min))
+    need("g", e_ob)
+    send(own_helper[p], "ob", T.offb[:], T.offb[:], own_mask)
+    e_off = ev(v.tensor_scalar(T.offs[:, p * TC:(p + 1) * TC], own_list, c0, float(PAD + R), OP.add, OP.min))
 
-    def clip(l):
-        r = who[l]
-        if r == p:
-            need("v", e_u)
-        else:
-            v.wait_ge(T.sem["al%d" % r], engines(list_mask(r)))
-        e_off[l] = ev(v.tensor_scalar(T.offs[:, r * TC:(r + 1) * TC], T.lists[:, r * TC:(r + 1) * TC],
-                                      float(PAD - R * p), float(PAD + R), OP.add, OP.min))
+    e_early = []
+    for q, name, (a, b) in ((s, "s", EARLY_S), (v, "v", EARLY_V)):
+        need(name, e_oa, e_ta, e_pad[0])
+        out, src = T.gat[:, p * TL + a:p * TL + b], T.win[:, 0:PAD + CA].indirect(T.offa[:, a // 16:b // 16])
+        e_early.append(ev(v.tensor_copy(out, src) if name == "v" else s.activation(out, src, COPY)))
 
-    clip(3)
-    e_low = ev(v.tensor_scalar(T.low[:], T.low0[:], 1e6, None, OP.mult))
-    e_z = ev(v.memset(T.scn[:, 15:16], 0.0))
-    e_mz = ev(v.memset(mz(0, HEAD, TL), 0.0))
-    need("v", e_cu, e_low, e_mz)
-    e_mo = mark(0, p)
-    for l in range(3):
-        clip(l)
-
-    e_g = {}
+    e_g, arrived = {}, {}
 
     def gath(name, l, a, b):
         r = who[l]
-        need(name, e_off[l], e_tab, *e_pad)
+        if l == 3:
+            need(name, e_off)
+        elif (name, l) not in arrived:
+            arrived[(name, l)] = 1
+            {"v": v, "s": s}[name].wait_ge(T.sem["al%d" % r], engines(lanes(r, list_users(r), core)))
+        need(name, e_tb, *e_pad)
         out = T.gat[:, r * TL + a:r * TL + b]
         src = T.win[:].indirect(T.offs[:, r * TC + a // 16:r * TC + b // 16])
         e_g[(l, a, b)] = ev(v.tensor_copy(out, src) if name == "v" else s.activation(out, src, COPY))
 
     for x in PLAN_S:
         gath("s", *x)
+    last = []
     for x in PLAN_V:
+        if x[0] == 3 and not last:
+            v.wait_ge(T.sem.am, engines(near_mask(p)))
+            last = scan_of(0, p, 0, HEAD, e_early, last)
         gath("v", *x)
     for i, (l, a, b) in enumerate(SENDS):
-        need("g", e_g[(l, a, b)])
+        need("g", *[e_g[k] for k in sorted(e_g) if k[0] == l and a <= k[1] < b])
         ap = T.gat[:, who[l] * TL + a:who[l] * TL + b]
         send(helper_for(l), "ag%d" % i, ap, ap, piece_mask(l))
+        if i == PUSH:
+            need("g", e_tb)
+            send(own_helper[p], "ow", T.win[:, PAD:PAD + CB], T.win[:, PAD + CA:PAD + R], own_mask)
 
-    v.wait_ge(T.sem.ao, engines(common(near_helper[p], [core, T.cores[nr]])))
-    last = []
-    for a, b in sorted([(a, b) for (l, a, b) in PLAN_S + PLAN_V if l == 3 and a >= HEAD]):
-        last = scan(0, p, a, b, [e_g[(3, a, b)], e_mo], last)
+    for k in sorted(k for k in e_g if k[0] == 3):
+        last = scan_of(0, p, k[1], k[2], [e_g[k]], last)
+    v.wait_ge(T.sem.ao, engines(back_mask))
+    need("s", e_cu)
+    e_a = picks(0, p, last + [e_z], 0, T.acc, T.lando)
+    need("v", *e_a)
     v.wait_ge(T.sem.af, engines(common(far_helper[f2], [core, far_helper[f1]])))
-    need("v", *last, e_z)
-    e_a = ev(v.tensor_tensor(T.acc[:], bags(0, p), T.landf[:], OP.max))
-    need("v", e_a)
-    v.wait_ge(T.sem.an, engines(common(near_helper[nr], [core, T.cores[nr]])))
-    e_y = ev(v.tensor_tensor(T.yt[:], T.acc[:], T.landn[:], OP.max))
+    e_b = ev(v.tensor_tensor(T.pre[:], T.acc[:], T.landf[:], OP.max))
+    need("v", e_b)
+    v.wait_ge(T.sem.an, engines(near_mask(nr)))
+    e_y = ev(v.tensor_tensor(T.yt[:], T.pre[:], T.landn[:], OP.max))
     need("y", e_y)
     e_o = ev(sy.dma_start(T.y[:], T.yt[:]), 16)
     need("y", e_o)

from concourse.bass import DstId, RemoteDMATransfer
from concourse.mybir import dt, AluOpType, AxisListType, ActivationFunctionType

N, R, TL, B = 4, 16384, 4096, 512
WORLD = 256
TC, BC = TL // 16, B // 16
PAD = 16
WW = R + 2 * PAD
CA = 14336
CB = R - CA
MW = TL + B
SW = TL + 16
NEV = 100
HEAD = 2560
HC = HEAD // 16
EARLY_S, EARLY_V = (0, 1312), (1312, 2560)
OWN_S = 1280
PUSH = 0
PLAN_S = [(0, 0, 1024), (0, 2048, 3072), (1, 0, 1024), (1, 2048, 3072), (2, 0, 768), (2, 1536, 2304), (2, 3072, 3584),
          (3, 2560, 3328), (3, 3328, 3712), (3, 3904, 4096)]
PLAN_V = [(0, 1024, 2048), (0, 3072, 4096), (1, 1024, 2048), (1, 3072, 4096), (2, 768, 1536), (2, 2304, 3072), (2, 3584, 4096),
          (3, 3712, 3904)]
SENDS = [(0, 0, 2048), (0, 2048, 4096), (1, 0, 2048), (1, 2048, 4096), (2, 0, 1536), (2, 1536, 3072), (2, 3072, 4096)]

SCRATCH = {
    "lraw": ("sbuf", [128, TC + BC], "int32"),
    "lf": ("sbuf", [128, TC + 1 + BC], "float32"),
    "fa": ("sbuf", [128, HC], "float32"),
    "fb": ("sbuf", [128, HC], "float32"),
    "cf": ("sbuf", [128, 2 * BC], "float32"),
    "flag": ("sbuf", [128, BC], "float32"),
    "spare0": ("sbuf", [128, BC], "float32"),
    "spare": ("sbuf", [128, BC], "float32"),
    "ones": ("sbuf", [128, 128], "float32"),
    "rep": ("sbuf", [128, 128], "float32"),
    "sh1": ("sbuf", [128, 128], "float32"),
    "sh2": ("sbuf", [128, 128], "float32"),
    "ps": ("psum", [128, 512], "float32"),
    "ps2": ("psum", [128, 512], "float32"),
    "ps3": ("psum", [128, 512], "float32"),
    "lists": ("sbuf", [128, N * TC], "uint16"),
    "cuts": ("sbuf", [128, N * 2 * BC], "uint16"),
    "offs": ("sbuf", [128, N * TC], "uint16"),
    "offa": ("sbuf", [128, HC], "uint16"),
    "offb": ("sbuf", [128, HC], "uint16"),
    "low0": ("sbuf", [128, B], "bfloat16"),
    "low": ("sbuf", [128, B], "bfloat16"),
    "win": ("sbuf", [128, WW], "bfloat16"),
    "msk": ("sbuf", [128, 2 * MW], "bfloat16"),
    "gat": ("sbuf", [128, N * TL], "bfloat16"),
    "scn": ("sbuf", [128, 2 * SW], "bfloat16"),
    "part": ("sbuf", [128, 2 * B], "bfloat16"),
    "pick": ("sbuf", [128, B], "bfloat16"),
    "landn": ("sbuf", [128, B], "bfloat16"),
    "landf": ("sbuf", [128, B], "bfloat16"),
    "lando": ("sbuf", [128, B], "bfloat16"),
    "pre": ("sbuf", [128, B], "bfloat16"),
    "acc": ("sbuf", [128, B], "bfloat16"),
    "yt": ("sbuf", [128, B], "bfloat16"),
}
SEMAPHORES = (["e%d" % i for i in range(NEV)] + ["al%d" % i for i in range(N)] + ["ac%d" % i for i in range(N)]
              + ["ag%d" % i for i in range(len(SENDS))] + ["an", "af", "ao", "am", "ob", "ow", "sent"])


def engines(mask):
    return bin(mask).count("1")


def rank_program(g, core, T, topo):
    def helpers_of(r):
        c0 = T.cores[r]
        return [c for c in range(WORLD) if topo.host(c) == topo.host(c0) and topo.chip(c) == topo.chip(c0)
                and topo.die(c) == topo.die(c0) and T.rank_of(c) is None][0:3]

    far_helper = [helpers_of(r)[0] for r in range(N)]
    near_helper = [helpers_of(r)[1] for r in range(N)]
    own_helper = [helpers_of(r)[2] for r in range(N)]
    crews = {"rank": T.cores, "far": far_helper, "near": near_helper, "own": own_helper}
    mine = [k for k in crews if core in crews[k]]
    if not mine:
        return
    role = mine[0]
    p = crews[role].index(core)

    def around(q):
        others = [r for r in range(N) if r != q]
        fa = [r for r in others if topo.host(T.cores[r]) != topo.host(T.cores[q])]
        fa = sorted(fa, key=lambda r: topo.die(T.cores[r]) == topo.die(T.cores[q]))
        return fa + [r for r in others if r not in fa]

    f1, f2, nr = around(p)
    who = [f1, f2, nr, p]
    v, s, te, sy = g.vector, g.scalar, g.tensor, g.sync
    OP, COPY = AluOpType, ActivationFunctionType.Copy

    n_ev, waited, all_ev, seen, nsent = [0], {}, [], {}, [0]

    def ev(inst, n=1):
        sem = T.sem["e%d" % n_ev[0]]
        n_ev[0] += 1
        inst.then_inc(sem, n)
        e = (n_ev[0], sem, n)
        all_ev.append(e)
        return e

    def need(name, *evs):
        q = {"v": v, "s": s, "t": te, "y": sy, "g": g}[name]
        for e in evs:
            if (name, e[0]) not in seen:
                seen[(name, e[0])] = 1
                waited[e[0]] = 1
                q.wait_ge(e[1], e[2])

    def finish():
        g.wait_ge(T.sem.sent, nsent[0])
        for e in all_ev:
            if e[0] not in waited:
                need("g", e)

    def common(src, dsts):
        m = 0xFFFF
        for d in dsts:
            m &= topo.mask(src, d)
        return m

    def put(dsts, sem, ap, mask):
        ids = []
        for d in dsts:
            rid, pid = topo.addr(d, core)
            ids.append(DstId(rid=rid, pnc=pid))
        g.remote_dma_fused([RemoteDMATransfer(srcs=[ap], dsts=[ap for d in dsts], dst_ids=ids, dma_engine_mask=mask,
                                              remote_sem=T.sem[sem])], local_sem=T.sem.sent)
        nsent[0] += engines(mask)

    def send(dst, sem, out, in_, mask):
        rid, pid = topo.addr(dst, core)
        g.remote_dma(out_ap=out, in_ap=in_, remote_sem=T.sem[sem], local_sem=T.sem.sent, pid=pid, routing_id=rid,
                     dma_engine_mask=mask)
        nsent[0] += engines(mask)

    def lanes(r, users, dst):
        away = [d for d in users if topo.chip(d) != topo.chip(T.cores[r]) or topo.host(d) != topo.host(T.cores[r])]
        out = common(T.cores[r], away)
        return out if dst in away else topo.mask(T.cores[r], dst) & ~out

    def give(r, users, sem, ap):
        for m in sorted(set(lanes(r, users, d) for d in users)):
            put([d for d in users if lanes(r, users, d) == m], sem, ap, m)

    def cut_users(r):
        a, b, c = around(r)
        return [near_helper[r], near_helper[c], own_helper[r], far_helper[a], far_helper[b]]

    def list_users(r):
        return [T.cores[q] for q in range(N) if q != r]

    def cuts_here(r):
        for q in (v, s):
            q.wait_ge(T.sem["ac%d" % r], engines(lanes(r, cut_users(r), core)))

    H = BC // 2
    HB = B // 2

    def ends(r, h):
        o = 2 * BC * r + h * H
        return T.cuts[:, o:o + H]

    def starts(r):
        return T.cuts[:, 2 * BC * r + BC:2 * BC * (r + 1)]

    def mz(k, a=0, b=TL):
        return T.msk[:, k * MW + a:k * MW + b]

    def mark(k, r):
        return ev(v.tensor_copy(T.msk[:, k * MW:(k + 1) * MW].indirect(starts(r)), T.low[:]))

    def scan_of(k, r, a, b, deps, last):
        need("v", *deps)
        o = k * SW + 16
        init = -9e29
        if a:
            need("v", *last)
            init = T.scn[:, o + a - 1:o + a]
        return [ev(v.tensor_tensor_scan(T.scn[:, o + a:o + b], mz(k, a, b), T.gat[:, r * TL + a:r * TL + b], init,
                                        OP.add, OP.max))]

    def bags(k, r, h):
        return T.scn[:, k * SW + 15:(k + 1) * SW].indirect(ends(r, h))

    def half(t, h, k=0):
        return t[:, k * B + h * HB:k * B + (h + 1) * HB]

    def picks(k, r, deps, out_k, out, other=None):
        need("v", *deps)
        need("s", *deps)
        if other is None:
            return [ev(v.tensor_copy(half(out, 0, out_k), bags(k, r, 0))),
                    ev(s.activation(half(out, 1, out_k), bags(k, r, 1), COPY))]
        e_s = ev(s.activation(half(T.pick, 1), bags(k, r, 1), COPY))
        e = [ev(v.tensor_tensor(half(out, 0, out_k), bags(k, r, 0), half(other, 0), OP.max))]
        need("v", e_s)
        return e + [ev(v.tensor_tensor(half(out, 1, out_k), half(T.pick, 1), half(other, 1), OP.max))]

    def low_columns():
        e = ev(v.memset(T.low0[:], -9e29))
        need("v", e)
        return ev(v.tensor_scalar(T.low[:], T.low0[:], 1e6, None, OP.mult))

    def helper_for(l):
        return (far_helper if l < 2 else near_helper)[p]

    def piece_mask(l):
        return topo.mask(T.cores[p], helper_for(l))

    def scan_pieces(k, l, e_k):
        last = []
        for i, (m, a, b) in enumerate(SENDS):
            if m == l:
                v.wait_ge(T.sem["ag%d" % i], engines(piece_mask(l)))
                last = scan_of(k, who[l], a, b, [e_k], last)
        return last

    own_mask = topo.mask(T.cores[p], own_helper[p])
    back_mask = topo.mask(own_helper[p], T.cores[p])

    def near_mask(q):
        return common(near_helper[q], [T.cores[q], T.cores[around(q)[2]]])

    if role == "far":
        mate = far_helper[nr]
        pm = common(core, [T.cores[f2], mate])
        mate_pm = common(mate, [T.cores[f1], core])
        e_z = [ev(v.memset(T.scn[:, k * SW + 15:k * SW + 16], 0.0)) for k in range(2)]
        e_low = low_columns()
        e_m = [ev(v.memset(mz(k), 0.0)) for k in range(2)]
        e_k = []
        for k, r in enumerate((f1, f2)):
            cuts_here(r)
            need("v", e_m[k], e_low)
            e_k.append(mark(k, r))
        for k, r in enumerate((f1, f2)):
            last = scan_pieces(k, k, e_k[k])
            out = T.part[:, k * B:(k + 1) * B]
            if k == 0:
                e_p = picks(k, r, last + [e_z[k]], k, T.part)
                need("g", *e_p)
                send(mate, "an", T.landn[:], out, pm)
            else:
                v.wait_ge(T.sem.an, engines(mate_pm))
                e_p = picks(k, r, last + [e_z[k]], k, T.part, T.landn)
                need("g", *e_p)
                send(T.cores[r], "af", T.landf[:], out, pm)
        finish()
        return

    if role == "near":
        e_z = ev(v.memset(T.scn[:, 15:16], 0.0))
        e_low = low_columns()
        e_m = [ev(v.memset(mz(k), 0.0)) for k in range(2)]
        cuts_here(p)
        need("v", *e_m, e_low)
        e_k = mark(1, p)
        need("g", e_k)
        send(T.cores[p], "am", mz(0), mz(1), near_mask(p))
        cuts_here(nr)
        last = scan_pieces(0, 2, mark(0, nr))
        e_p = picks(0, nr, last + [e_z], 0, T.part)
        need("g", *e_p)
        send(T.cores[nr], "an", T.landn[:], T.part[:, 0:B], near_mask(p))
        finish()
        return

    if role == "own":
        e_z = ev(v.memset(T.scn[:, 15:16], 0.0))
        e_low = low_columns()
        need("v", e_low)
        e_pad = [ev(v.tensor_copy(T.win[:, 0:PAD], T.low[:, 0:PAD])),
                 ev(v.tensor_copy(T.win[:, PAD + CB:CB + 2 * PAD], T.low[:, 0:PAD]))]
        e_m = ev(v.memset(mz(0), 0.0))
        need("s", e_low)
        o = p * TL
        e_fill = [ev(s.activation(T.gat[:, o + a:o + a + B], T.low[:], COPY)) for a in range(HEAD, TL, B)]
        cuts_here(p)
        need("v", e_m)
        e_k = mark(0, p)
        win = T.win[:, 0:CB + 2 * PAD]
        for q, name in ((v, "v"), (s, "s")):
            q.wait_ge(T.sem.ob, engines(own_mask))
            q.wait_ge(T.sem.ow, engines(own_mask))
            need(name, *e_pad)
        e_s = ev(s.activation(T.gat[:, o:o + OWN_S], win.indirect(T.offb[:, 0:OWN_S // 16]), COPY))
        e_v = ev(v.tensor_copy(T.gat[:, o + OWN_S:o + HEAD], win.indirect(T.offb[:, OWN_S // 16:HC])))
        last = scan_of(0, p, 0, OWN_S, [e_k, e_s], [])
        last = scan_of(0, p, OWN_S, HEAD, [e_v], last)
        last = scan_of(0, p, HEAD, TL, e_fill, last)
        e_p = picks(0, p, last + [e_z], 0, T.part)
        need("g", *e_p)
        send(T.cores[p], "ao", T.lando[:], T.part[:, 0:B], back_mask)
        finish()
        return

    LE = TC + 1
    e_idx = ev(sy.dma_start(T.lraw[0:16, 0:TC], T.idx[:]), 16)
    e_end = ev(s.dma_start(T.lraw[0:16, TC:TC + BC], T.end[:]), 16)
    e_ta = ev(sy.dma_start(T.win[:, PAD:PAD + CA], T.tab[:, 0:CA]), 16)
    e_tb = ev(sy.dma_start(T.win[:, PAD + CA:PAD + R], T.tab[:, CA:R]), 16)

    e_ones = ev(v.memset(T.ones[0:16, :], 1.0))
    e_z0 = ev(v.memset(T.lf[0:16, TC:TC + 1], 0.0))
    need("g", e_ones)
    e_rep = ev(g.affine_select(T.rep[0:16, :], T.ones[0:16, :], [[0, 8], [1, 16]], OP.is_equal, 0.0, 0, -1))
    e_sp = ev(g.iota(T.spare0[0:16, :], [[16, BC]], TL, 1, allow_small_or_imprecise_dtypes=True))
    e_s1 = ev(g.affine_select(T.sh1[0:16, :], T.ones[0:16, :], [[0, 8], [1, 16]], OP.is_equal, 0.0, -1, -1))
    e_s2 = ev(g.affine_select(T.sh2[0:16, :], T.ones[0:16, :], [[0, 8], [1, 16]], OP.is_equal, 0.0, 15, -1))
    e_low0 = ev(v.memset(T.low0[:, 0:PAD], -9e29))
    need("v", e_low0)
    e_pad = [ev(v.tensor_scalar(T.win[:, 0:PAD], T.low0[:, 0:PAD], 1e6, None, OP.mult)),
             ev(v.tensor_scalar(T.win[:, PAD + R:WW], T.low0[:, 0:PAD], 1e6, None, OP.mult))]
    e_z = ev(v.memset(T.scn[:, 15:16], 0.0))

    need("v", e_idx)
    e_c = ev(v.tensor_copy(T.lf[0:16, 0:TC], T.lraw[0:16, 0:TC]))
    need("v", e_end)
    e_c2 = ev(v.tensor_copy(T.lf[0:16, LE:LE + BC], T.lraw[0:16, TC:TC + BC]))
    need("t", e_rep, e_c)
    e_ps = ev(te.matmul(T.ps[:, 0:TC], T.rep[0:16, :], T.lf[0:16, 0:TC], start=True, stop=True))
    need("t", e_sp)
    e_ps3 = ev(te.matmul(T.ps3[:, 0:BC], T.rep[0:16, :], T.spare0[0:16, :], start=True, stop=True))
    need("t", e_c2, e_s1, e_s2, e_z0)
    E, EP = T.lf[0:16, LE:LE + BC], T.lf[0:16, TC:TC + BC]
    e_ps2 = [ev(te.matmul(T.ps2[:, 0:BC], T.rep[0:16, :], E, start=True, stop=True))]
    te.matmul(T.ps2[:, BC:2 * BC], T.sh1[0:16, :], E, start=True, stop=False)
    e_ps2.append(ev(te.matmul(T.ps2[:, BC:2 * BC], T.sh2[0:16, :], EP, start=False, stop=True)))
    need("v", e_ps)
    own_list = T.lists[:, p * TC:(p + 1) * TC]
    e_u = ev(v.tensor_copy(own_list, T.ps[:, 0:TC]))
    need("v", e_u)
    for q in (f1, f2, nr):
        out = T.lists[:, q * TC:(q + 1) * TC]
        e_l = ev(v.tensor_scalar(out, own_list, float(PAD - R * q), float(PAD + R), OP.add, OP.min))
        need("g", e_l)
        send(T.cores[q], "al%d" % p, T.offs[:, p * TC:(p + 1) * TC], out, lanes(p, list_users(p), T.cores[q]))

    c0 = float(PAD - R * p)
    raw = T.ps[:, 0:HC]
    e_fa = ev(v.tensor_scalar(T.fa[:], raw, c0, float(PAD + CA), OP.add, OP.is_lt))
    e_fb = ev(v.tensor_scalar(T.fb[:], raw, c0, None, OP.add))
    need("v", e_ps3)
    e_d = ev(v.tensor_copy(T.spare[:], T.ps3[:, 0:BC]))
    need("v", e_fa, e_fb)
    e_fm = ev(v.tensor_tensor(T.fa[:], T.fa[:], T.fb[:], OP.mult))
    need("v", *e_ps2)
    e_cf = ev(v.tensor_copy(T.cf[:], T.ps2[:, 0:2 * BC]))
    need("v", e_fm)
    e_oa = ev(v.tensor_copy(T.offa[:], T.fa[:]))

    F, D, CE, CS = T.flag[:], T.spare[:], T.cf[:, 0:BC], T.cf[:, BC:2 * BC]
    need("v", e_cf, e_d)
    e_f = ev(v.tensor_tensor(F, CE, CS, OP.is_gt))
    e_2 = ev(v.tensor_tensor(CS, CS, D, OP.subtract))
    need("v", e_f, e_2)
    e_1 = ev(v.tensor_tensor(CE, CE, F, OP.mult))
    e_3 = ev(v.tensor_tensor(CS, CS, F, OP.mult))
    need("v", e_1, e_3)
    e_4 = ev(v.tensor_tensor(CS, CS, D, OP.add))
    need("v", e_4)
    own_cuts = T.cuts[:, 2 * BC * p:2 * BC * (p + 1)]
    e_cu = ev(v.tensor_copy(own_cuts, T.cf[:]))
    need("g", e_cu)
    give(p, cut_users(p), "ac%d" % p, own_cuts)

    e_ob = ev(v.tensor_scalar(T.offb[:], raw, c0 - CA, float(PAD + CB), OP.add, OP.min))
    need("g", e_ob)
    send(own_helper[p], "ob", T.offb[:], T.offb[:], own_mask)
    e_off = ev(v.tensor_scalar(T.offs[:, p * TC:(p + 1) * TC], own_list, c0, float(PAD + R), OP.add, OP.min))

    e_early = []
    for q, name, (a, b) in ((s, "s", EARLY_S), (v, "v", EARLY_V)):
        need(name, e_oa, e_ta, e_pad[0])
        out, src = T.gat[:, p * TL + a:p * TL + b], T.win[:, 0:PAD + CA].indirect(T.offa[:, a // 16:b // 16])
        e_early.append(ev(v.tensor_copy(out, src) if name == "v" else s.activation(out, src, COPY)))

    e_g, arrived = {}, {}

    def gath(name, l, a, b):
        r = who[l]
        if l == 3:
            need(name, e_off)
        elif (name, l) not in arrived:
            arrived[(name, l)] = 1
            {"v": v, "s": s}[name].wait_ge(T.sem["al%d" % r], engines(lanes(r, list_users(r), core)))
        need(name, e_tb, *e_pad)
        out = T.gat[:, r * TL + a:r * TL + b]
        src = T.win[:].indirect(T.offs[:, r * TC + a // 16:r * TC + b // 16])
        e_g[(l, a, b)] = ev(v.tensor_copy(out, src) if name == "v" else s.activation(out, src, COPY))

    for x in PLAN_S:
        gath("s", *x)
    last = []
    for x in PLAN_V:
        if x[0] == 3 and not last:
            v.wait_ge(T.sem.am, engines(near_mask(p)))
            last = scan_of(0, p, 0, HEAD, e_early, last)
        gath("v", *x)
    for i, (l, a, b) in enumerate(SENDS):
        need("g", *[e_g[k] for k in sorted(e_g) if k[0] == l and a <= k[1] < b])
        ap = T.gat[:, who[l] * TL + a:who[l] * TL + b]
        send(helper_for(l), "ag%d" % i, ap, ap, piece_mask(l))
        if i == PUSH:
            need("g", e_tb)
            send(own_helper[p], "ow", T.win[:, PAD:PAD + CB], T.win[:, PAD + CA:PAD + R], own_mask)

    for k in sorted(k for k in e_g if k[0] == 3):
        last = scan_of(0, p, k[1], k[2], [e_g[k]], last)
    v.wait_ge(T.sem.ao, engines(back_mask))
    need("s", e_cu)
    e_a = picks(0, p, last + [e_z], 0, T.acc, T.lando)
    need("v", *e_a)
    v.wait_ge(T.sem.af, engines(common(far_helper[f2], [core, far_helper[f1]])))
    e_b = ev(v.tensor_tensor(T.pre[:], T.acc[:], T.landf[:], OP.max))
    need("v", e_b)
    v.wait_ge(T.sem.an, engines(near_mask(nr)))
    e_y = ev(v.tensor_tensor(T.yt[:], T.pre[:], T.landn[:], OP.max))
    need("y", e_y)
    e_o = ev(sy.dma_start(T.y[:], T.yt[:]), 16)
    need("y", e_o)
    finish()
